import numpy as np, ml_dtypes
CORES = [6,15,38,47]
N = 4
import mx_ref
BF = ml_dtypes.bfloat16
def gentries(a):
    return np.ascontiguousarray(a.reshape(8, 16, -1).transpose(0, 2, 1)).reshape(8, -1)
def gtable(e):
    e = np.asarray(e); return np.ascontiguousarray(e.reshape(8, -1, 16).transpose(0, 2, 1)).reshape(128, -1).astype(np.int32)
def gcols(t, e):
    v = np.concatenate([t.reshape(8, 16, -1, 4), np.zeros((8, 16, 1, 4), BF)], axis=2)
    return np.ascontiguousarray(np.stack([v[g][:, e[g]] for g in range(8)])).reshape(128, -1)
def gpick(z, e):
    return np.concatenate([z[16 * g:16 * g + 16][:, e[g]] for g in range(8)])
def tile(rs):
    return np.stack(rs, axis=2).reshape(128, -1).astype(BF)
def pick(q, e):
    c = np.concatenate([q[0].reshape(128, -1, 4), np.zeros((128, 1, 4), np.uint8)], axis=1); s = np.concatenate([q[1], np.ones((16, 1), np.uint8)], axis=1)
    return (np.ascontiguousarray(c[:, e].reshape(128, -1)), np.ascontiguousarray(s[:, e]))
def join(*qs):
    return (np.concatenate([q[0] for q in qs], axis=1), np.concatenate([q[1] for q in qs], axis=1))
def put(q, e, v):
    c, s = q[0].reshape(128, -1, 4).copy(), q[1].copy(); c[:, e] = v[0].reshape(128, -1, 4); s[:, e] = v[1]
    return (c.reshape(128, -1), s)
def pk(c, s):
    return (np.ascontiguousarray(c), mx_ref.live(s))
def emit(q):
    return q[0], q[1]
def packed(v, rng):
    q = [mx_ref.quantize(np.ascontiguousarray(v[r])) for r in range(N)]
    return np.stack([a for a, b in q]), np.stack([mx_ref.plane(b, rng) for a, b in q])
def values_of_codes():
    e, c = np.zeros((128, 128, 4), np.float32), np.zeros((128, 2, 4), np.uint8)
    e[np.arange(128), np.arange(128), 0] = 1
    c[:127, :, 0] = np.arange(256).reshape(2, 128).T[:127]
    return mx_ref.matmul(mx_ref.quantize(e.reshape(128, 512).astype(BF)), (c.reshape(128, 8), np.full((16, 2), 127, np.uint8))).T.reshape(-1).astype(np.float64)
CODE_VALUE, SCALE_VALUE = values_of_codes(), 2.0 ** (np.arange(256) - 127.0)
def decode(q):
    return (CODE_VALUE[q[0]].reshape(16, 8, -1, 4) * SCALE_VALUE[q[1]][:, None, :, None] + 0.0).reshape(128, -1).astype(np.float32)
def f(rng, *shape):
    return mx_ref.flush((rng.standard_normal(shape, dtype=np.float32) * np.exp2(rng.integers(-2, 3, shape[:-1] + (1,)))).astype(BF))
def wide(rng, *shape, cols=0):
    v = rng.standard_normal(shape, dtype=np.float32) * np.exp2(rng.integers(-12, 13, shape)).astype(np.float32)
    if cols: v *= np.repeat(np.exp2(rng.integers(-cols, cols + 1, shape[:-2] + (1, shape[-1] // 4))) * (rng.random(shape[:-2] + (1, shape[-1] // 4)) > 0.0625), 4, axis=-1).astype(np.float32)
    return mx_ref.flush(v.astype(BF))
C, L, M, R = 384, 5, 64, 3
def big(v):
    v = v.astype(np.float32)
    v[np.abs(v) < np.float32(2.0 ** -16)] = 0
    return v.astype(BF)
def numbers_of(rng):
    return {"x": big(f(rng, N, 128, 4 * C)), "u": np.array(f(rng, N, 128, 512)), "v": np.array(f(rng, N, 128, 512))}
def some_links(rng):
    w = rng.choice([8, 16, 32, C], (8, 1, 1))
    return (np.arange(C) + 1 + (rng.random((8, 2, C)) * w).astype(np.int64)) % C
def links_of(rng):
    return np.stack([gtable(some_links(rng).reshape(8, 2 * C)) for r in range(N)])
def layers(rng):
    return big(f(rng, N, 128, 2048)).reshape(N, 8, 16, 4, 8, 16, 4)
def weights(rng, w):
    c, p = packed(np.ascontiguousarray(w).reshape(N, 128, 2048), rng)
    return {"wc": c, "ws": p}
def setup_inputs(rng):
    return {**numbers_of(rng), "nb": links_of(rng), **weights(rng, layers(rng))}
def setup_inputs_ties(rng):
    d = numbers_of(rng)
    o = rng.permutation(N)
    k = rng.integers(-1, 3, (N, 8, C))
    k[o[1]] = rng.integers(-3, 0, (8, C))
    k[o[2]] = 1
    x = d["x"].reshape(N, 8, 16, C, 4)
    x[:, :, 0] = 0
    x[:, :, 0, :, 0] = k.astype(np.float32).astype(BF)
    u = d["u"].reshape(N, 128, 128, 4)
    u[:, :, ::16] = 0
    for h in range(0, 128, 16): u[:, h, h, 0] = 1
    u[o[0], :, ::16] = 0
    w = layers(rng)
    w[:, :, :, :, :, 0] = 0
    return {"x": x.reshape(N, 128, 4 * C), "u": u.reshape(N, 128, 512), "v": d["v"], "nb": links_of(rng), **weights(rng, w)}
def setup_inputs_near(rng):
    d = numbers_of(rng)
    x = d["x"].astype(np.float32).reshape(N, 8, 16, C, 4)
    x[:, :, 0] = 0
    x[:, :, 8:] = 0
    s = rng.integers(0, 16, (N, 8, C))
    s = ((s[:, :, :, None] >> np.arange(4)) & 1) * np.exp2(np.arange(4) - 23.0)
    u = d["u"].reshape(N, 128, 128, 4)
    u[:, :, ::16] = 0
    nb = np.stack([some_links(rng) for r in range(N)])
    n = np.arange(C)
    first = n // 3 * 3 % (C - C % 3)
    o = rng.permutation(N) % 4
    for r in range(N):
        k = 1.0 if o[r] == 0 else 2.0 ** -30
        if o[r] < 2:
            x[r, :, 0, :, 0] = rng.choice([-1.0, 1.0], (8, C))
            x[r, :, 11, :, 0] = 2.0 ** -10
            x[r, :, 8] = s[r]
            g, e = rng.integers(8), rng.permutation(C)
            nb[r, g, 0, e], nb[r, g, 1, e] = e[first + (n + 1) % 3], e[first + (n + 2) % 3]
            x[r, g, 0, C - 1, 0] = 1.0
            x[r, g, 8, C - 1] = np.exp2(np.arange(4) - 23.0)
        elif o[r] == 2:
            x[r, :, 8, :, 0] = rng.integers(-1, 3, (8, C)) * 2.0 ** -29
            for g in rng.permutation(8)[:4]: x[r, g, 8, rng.integers(C), 0] = rng.choice([-1.0, 1.0]) * 2.0 ** 29
        else:
            x[r, :, 0, :, 0] = rng.choice([0.0, 0.0, 0.0, 0.0, 0.0, 0.0, 1.0, -1.0], (8, C))
            x[r, :, 8] = s[r] * rng.choice([-1.0, 1.0], (8, C, 1))
        for h in range(0, 128, 16):
            u[r, h, h, 0] = 1.0 if o[r] == 3 else 0.0 if o[r] == 2 else k
            u[r, h + 8, h] = k
            if o[r] < 2: u[r, h + 11, h, 0] = k
    w = layers(rng)
    for i in [0, 8, 9, 10, 11, 12, 13, 14, 15]:
        w[:, :, i] = 0
        w[:, :, :, :, :, i] = 0
    return {"x": x.reshape(N, 128, 4 * C).astype(BF), "u": u.reshape(N, 128, 512), "v": d["v"], "nb": np.stack([gtable(nb[r].reshape(8, 2 * C)) for r in range(N)]), **weights(rng, w)}
def setup_inputs_huge(rng):
    d = numbers_of(rng)
    c = rng.choice([-1.0, 1.0], (N, 1, C, 1))
    c[rng.permutation(N)[:N // 2]] = -1.0
    x = 2.0 ** 30 * (0.6 + 0.2 * rng.random((N, 128, C, 4))) * c
    u = d["u"].reshape(N, 128, 128, 4)
    u[:, :, ::16] = (2.0 ** 30 * (1.0 - 0.1 * rng.random((N, 128, 8, 4)))).astype(np.float32).astype(BF)
    w = np.zeros((N, 128, 4, 128, 4), np.float32)
    i = np.arange(128)
    for b in range(4): w[:, i, b, i, b] = -2
    return {"x": x.astype(np.float32).reshape(N, 128, 4 * C).astype(BF), "u": u.reshape(N, 128, 512), "v": d["v"], "nb": links_of(rng), **weights(rng, w.astype(BF))}
def setup_inputs_forms(rng):
    d = numbers_of(rng)
    x = d["x"].astype(np.float32).reshape(N, 8, 16, C, 4)
    a = (1.0 + (2 * rng.integers(0, 64, (N, 8, 8, C, 4)) + 1) * 2.0 ** -7) * np.exp2(-rng.integers(8, 14, (N, 8, 8, C, 4)).astype(np.float64))
    x[:, :, :8] = a * rng.choice([-1.0, 1.0], a.shape)
    x[:, :, 0, :, 0] = rng.choice([1.875, 1.96875], (N, 8, C))
    x[:, :, 1, :, 0] = rng.integers(8, 10, (N, 8, C)) * rng.choice([-1.0, 1.0], (N, 8, C)) * 2.0 ** -16
    u = d["u"].reshape(N, 128, 128, 4)
    u[:, :, ::16] = 0
    for h in range(0, 128, 16): u[:, h + 1, h, 0] = 1
    nb = np.stack([some_links(rng) for r in range(N)])
    o = rng.permutation(N) % 4
    for r in range(N):
        count = rng.permutation([M, M, M, M - 1, M + 1, 1, 0, C])
        for g in range(8):
            if o[r] == 0: nb[r, g, 1] = nb[r, g, 0]
            if o[r] in (1, 2):
                n = rng.integers(0, 2 * L - 1, C)
                n[:2 * L - 2] = np.arange(1, 2 * L - 1)
                n[2 * L - 2] = 2 * L - 2
                if o[r] == 1: n[L - 2] = 2 * L - 2
                else: n[2 * L - 3] = 0
                m = n.copy()
                e = 2 * L - 1 + np.arange(min(int(count[g]), C - 2 * L + 1))
                if o[r] == 1: n[e] = rng.integers(0, 2, len(e)) * (L - 1)
                else: n[e] = rng.integers(0, 2 * L - 2, len(e))
                m[e] = (n[e] + L - 1) % (2 * L - 2)
                k = rng.permutation(C)
                nb[r, g, 0, k], nb[r, g, 1, k] = k[n], k[m]
    return {"x": x.reshape(N, 128, 4 * C).astype(BF), "u": u.reshape(N, 128, 512), "v": d["v"], "nb": np.stack([gtable(nb[r].reshape(8, 2 * C)) for r in range(N)]), **weights(rng, layers(rng))}
def setup_inputs_spread(rng):
    d = setup_inputs(rng)
    d["x"] = big(wide(rng, N, 128, 4 * C, cols=6))
    return d
def check_inputs(d):
    b = []
    for k in ("x", "u", "v"):
        a = np.abs(d[k].astype(np.float32))
        if not (np.isfinite(a).all() and ((a == 0) | (a >= 2.0 ** -30) & (a <= 2.0 ** 30)).all()): b.append("a value of " + k)
    if not ((d["nb"] >= 0) & (d["nb"] < C)).all(): b.append("an entry of nb")
    none, least, most = [emit(mx_ref.quantize(np.full((128, 16), k, np.float32).astype(BF)))[1][0, 0] for k in (0.0, 2.0 ** -30, 2.0 ** 30)]
    for r in range(N):
        if ((d["wc"][r] == 0x7F) | (d["wc"][r] == 0xFF)).any(): b.append("wc: a code that is no number")
        s = mx_ref.live(d["ws"][r])
        if ((s != none) & ((s < least) | (s > most))).any(): b.append("ws: a scale out of range")
    return b
def bubbles(a, s):
    at = lambda t, e: np.take_along_axis(t, e, axis=1)
    c = np.where(s > 0, a[:, C:], a[:, :C])
    p, q = [a[:, :C]], [a[:, C:]]
    for k in range(1, L):
        p.append(at(c, p[-1]))
        q.append(at(c, q[-1]))
    i, j = np.full((8, C), -1), np.full((8, C), -1)
    for n in reversed(range(2 * L - 1)):
        for k in reversed(range(max(0, n - L + 1), min(n, L - 1) + 1)):
            met = p[k] == q[n - k]
            i[met], j[met] = k, n - k
    is_bubble = (i >= 0) & (p[0] != q[0])
    o = np.lexsort((-s, ~is_bubble))[:, :M]
    filled = at(is_bubble, o)
    g, k = np.arange(8)[:, None, None], np.arange(L)
    np0 = np.stack(p, axis=2)[g, o[:, :, None], np.minimum(k, at(i, o)[:, :, None])]
    nq0 = np.stack(q, axis=2)[g, o[:, :, None], np.minimum(k, at(j, o)[:, :, None])]
    one = at(s, at(q[0], o)) > at(s, at(p[0], o))
    new = a.copy()
    h, m = np.nonzero(filled)
    new[h, (o + C * ~one)[h, m]] = np0[h, m, L - 1]
    slots = [np.where(filled[:, :, None], t, -1).reshape(8, L * M) for t in (np0, nq0, np.where(one[:, :, None], nq0, np0))]
    e = np.full((8, C), -1)
    for n in reversed(range(L * M)):
        h = np.flatnonzero(slots[2][:, n] >= 0)
        e[h, slots[2][h, n]] = n
    return slots[0], slots[1], e, new
def reference(x, u, v, nb, wc, ws):
    qu = [mx_ref.quantize(u[r]) for r in range(N)]
    lay = [pk(wc[r], ws[r]) for r in range(N)]
    now = [x[r] for r in range(N)]
    links = [gentries(nb[r]).astype(np.int64) for r in range(N)]
    for t in range(R):
        own, sent, place = [], [], []
        for r in range(N):
            q = mx_ref.quantize(now[r])
            own.append(decode(q))
            s = mx_ref.matmul(qu[r], q)[::16] + np.float32(0.0)
            a, b, e, links[r] = bubbles(links[r], s)
            place.append(e)
            w = own[r].astype(BF)
            sent.append(mx_ref.quantize(((gcols(w, a).astype(np.float32) + gcols(w, b).astype(np.float32)) * np.float32(0.5)).astype(BF)))
        for r in range(N):
            came, made = sent[(r - 1) % N], []
            for b in range(4):
                h = mx_ref.matmul(pick(lay[r], np.arange(128 * b, 128 * b + 128)), came) * np.float32(0.03125)
                made.append(gpick(np.concatenate([h, np.zeros((128, 1), np.float32)], axis=1), place[r]) + own[r][:, b::4])
            now[r] = tile(made)
    y, ol = np.zeros((N, 128, C), np.float32), np.zeros((N, 8, 2 * C), np.float32)
    oc, osc = np.zeros((N, 128, 4 * C), np.uint8), np.zeros((N, 16, C), np.uint8)
    for r in range(N):
        q = mx_ref.quantize(now[r])
        y[r] = mx_ref.matmul(mx_ref.quantize(v[r]), q)
        ol[r] = links[r]
        oc[r], osc[r] = emit(q)
    return {"y": y, "ol": ol, "oc": oc, "osc": osc}

@@ -1,0 +1,467 @@
+from concourse.mybir import dt, AluOpType as O, ActivationFunctionType as AF
+
+N, C, L, M, R = 4, 384, 5, 64, 3
+SL = L * M
+HALF = SL // 2
+PAIRS = sorted(((i + j, i, j) for i in range(L) for j in range(L)))
+NB = len(PAIRS) + 2
+EB = SL + 2
+BIG = 1e29
+VROWS = 4
+
+F32, BF, I32, U16, F16, COD = "float32", "bfloat16", "int32", "uint16", "float16", "float8_e4m3fn_x4"
+SCRATCH, PLACE = {}, {}
+
+
+def _own(dtype, spec):
+    for item in spec.split():
+        name, cols = item.split(":")
+        SCRATCH[name] = ("sbuf", [128, int(cols)], dtype)
+
+
+def _pool(pool, dtype, spec):
+    at = 0
+    for item in spec.split():
+        name, cols = item.split(":")
+        PLACE[name] = (pool, at)
+        at += (int(cols) + 31) // 32 * 32
+    SCRATCH[pool] = ("sbuf", [128, at], dtype)
+
+
+_own(BF, "x0:1536 x1:1536 x2:1536 x3:1536 ut:512 vt:512 et:2048 ones:512 za:1280 zt0:640 zt1:640")
+_own(BF, "fb0:384 fb1:384 fb2:384 fb3:384 db0:400 db1:400 db2:400 db3:400")
+_own(F32, "hs0:328 hs1:328 hs2:328 hs3:328 lrep:768 ys:384")
+_own(I32, "nbl:48 nbw:768")
+for _n, _k in (("w", 512), ("v", 128), ("u0", 128), ("u", 128), ("e", 512), ("x", 384)):
+    _own(COD, "q%s:%d" % (_n, _k))
+    _own("uint8", "s%s:%d" % (_n, _k))
+for _t in range(R):
+    _own(COD, "zc%d:320 lc%d:320" % (_t, _t))
+    _own("uint8", "zs%d:320 ls%d:320" % (_t, _t))
+_pool("poolf", F32, "jm16:768 jz:768 md:768 r16:768 mk:384 d0f:384 idr:384 col:32 nl:24 nm:24 nbias:24 cc:20 cd:20 ce:20 "
+      "ltyp:768 ll:48 dl:24 lx:768 lsn:768 smd:384 sn:384 sm5:384 fl:24 fx:24 ix:24 cm:24 cl:24 v0:384 v1:384 v2:384 "
+      "v3:384 va:384 vb:384 gg:768 gt:768 ow:24 ms:384 mi:384 ff:384 cnt:24 rk:24 order:384 o1:64 ol:64 pm:64 qm:64 "
+      "km:64 pab:128 ht:384 htt:384 ab:128 w:320 pp:64 pe:320 pr:320 pl:320 ps:320 k1:64 kl:64 po:8 n64:320 tv:192")
+_pool("poolb", BF, "r16b:384 d1k:648 one6:1932 ne:648 st:648 ex:384 kr:384 ka:384 tm:384 eq:384 eqs:384 mm:2304 "
+      "junk:1536 xp:320 d0e:7728")
+_pool("pooli", I32, "pi:2 li:48 li2:24 li3:20 li4:24 li5:8 ca:20 cb:20 kai:64 jm:64 pi3:60 pri:320 xri:320")
+_pool("poolu", U16, "upl:8 inl:48 exr:24 exp:20 pz:20 px:20 lu:48 ixu:24 cu:24 rku:24 ou:4 xyu:40 eu:24 pu:4")
+_pool("poolh", F16, "ste:7728")
+PSUM = ("pS", "pF0", "pF1", "pF2", "pF3")
+for _n in PSUM:
+    SCRATCH[_n] = ("psum", [128, 512], F32)
+NDMA = 40
+SEMAPHORES = ["qv_", "qa_", "qt_", "qp_", "lsent"] + ["ar%d" % t for t in range(R)] + ["d%d" % k for k in range(NDMA)]
+
+
+def rank_program(g, core, T, topo):
+    rank = T.rank_of(core)
+    if rank is None:
+        return
+    nxt = T.cores[(rank + 1) % N]
+    rid, pid = topo.addr(nxt)[:2]
+    mask, width = topo.mask(core, nxt), len(topo.engines(core, nxt))
+
+    eng = {"v": g.vector, "a": g.scalar, "t": g.tensor, "p": g, "s": g.sync}
+    semof = {"v": "qv_", "a": "qa_", "t": "qt_", "p": "qp_"}
+    count, known = {}, {q: {} for q in eng}
+    clocks, hist = {}, {}
+    ndma = [0]
+
+    def need(q, src, val):
+        if known[q].get(src, 0) >= val:
+            return
+        eng[q].wait_ge(T.sem[src], val)
+        for s, n in clocks.get((src, val), {src: val}).items():
+            if n > known[q].get(s, 0):
+                known[q][s] = n
+
+    def meet(x, y):
+        return x[0] < y[1] and y[0] < x[1] and not (x[2] == y[2] and (x[0] - y[0]) % x[2])
+
+    def covers(x, y):
+        return x[0] <= y[0] and y[1] <= x[1] and (x[2] == 1 or x[2] == y[2] and (x[0] - y[0]) % x[2] == 0)
+
+    def order(q, reads, writes):
+        todo = {}
+        mine = semof.get(q)
+        for r, w in [(r, False) for r in reads] + [(r, True) for r in writes]:
+            for piece, src, val, wrote in hist.get(r[0], ()):
+                if meet(r[1:], piece) and (w or wrote or (r[0] in PSUM and src != mine)):
+                    todo[src] = max(todo.get(src, 0), val)
+        for src in sorted(todo, key=lambda s: s != mine):
+            need(q, src, todo[src])
+
+    def note(src, val, reads, writes):
+        for r in writes:
+            h = [x for x in hist.get(r[0], ()) if not covers(r[1:], x[0])]
+            hist[r[0]] = h + [(r[1:], src, val, True)]
+        for r in reads:
+            if r not in writes:
+                h = [x for x in hist.get(r[0], ()) if not (x[0] == r[1:] and x[1] == src and not x[3])]
+                hist[r[0]] = h + [(r[1:], src, val, False)]
+
+    def emit(q, fn, reads, writes):
+        order(q, reads, writes)
+        src = semof[q]
+        count[src] = count.get(src, 0) + 1
+        fn().then_inc(T.sem[src], 1)
+        clocks[(src, count[src])] = {**known[q], src: count[src]}
+        note(src, count[src], reads, writes)
+
+    def dma(q, out, in_):
+        order(q, in_[1], out[1])
+        src = "d%d" % ndma[0]
+        ndma[0] += 1
+        eng[q].dma_start(out[0], in_[0]).then_inc(T.sem[src], 16)
+        count[src] = 16
+        clocks[(src, 16)] = {**known[q], src: 16}
+        note(src, 16, in_[1], out[1])
+
+    def A(n, a, b, s=1):
+        buf, o = PLACE.get(n, (n, 0))
+        return (T[buf][:, o + a:o + b:s] if s > 1 else T[buf][:, o + a:o + b], [(n, a, b, s)])
+
+    def U8(n, a, b):
+        return (T[n][:, a:b].bitcast(dt.uint8), [(n, a, b, 1)])
+
+    def U32(n, a, b):
+        return (T[n][:, a:b].bitcast(dt.uint32), [(n, a, b, 1)])
+
+    def I(win, off):
+        return (win[0].indirect(off[0]), win[1] + off[1])
+
+    def ext(v):
+        return (v, [])
+
+    def ap(x):
+        return x[0] if isinstance(x, tuple) else x
+
+    def rd(*xs):
+        return [r for x in xs if isinstance(x, tuple) for r in x[1]]
+
+    V = g.vector
+
+    def tc(out, in_):
+        emit("v", lambda: V.tensor_copy(out[0], in_[0]), rd(in_), out[1])
+
+    def scatter(win, off, in_):
+        emit("v", lambda: V.tensor_copy(win[0].indirect(off[0]), in_[0]), rd(off, in_), win[1])
+
+    def tt(out, a, b, op):
+        emit("v", lambda: V.tensor_tensor(out[0], a[0], b[0], op), rd(a, b), out[1])
+
+    def ts(out, a, s1, op0, s2=None, op1=None):
+        if op1 is None:
+            emit("v", lambda: V.tensor_scalar(out[0], a[0], ap(s1), None, op0), rd(a, s1), out[1])
+        else:
+            emit("v", lambda: V.tensor_scalar(out[0], a[0], ap(s1), ap(s2), op0, op1), rd(a, s1, s2), out[1])
+
+    def scan(out, d0, d1, op0, op1):
+        emit("v", lambda: V.tensor_tensor_scan(out[0], d0[0], d1[0], 0.0, op0, op1), rd(d0, d1), out[1])
+
+    def turn(out, in_):
+        emit("v", lambda: V.transpose(out[0], in_[0]), rd(in_), out[1])
+
+    def fill(out, k):
+        emit("v", lambda: V.memset(out[0], k), [], out[1])
+
+    def quant(q, s, x):
+        emit("v", lambda: V.quantize_mx(q[0], s[0], x[0]), rd(x), q[1] + s[1])
+
+    def act(out, in_, func=AF.Copy, bias=None, scale=None, accum=None):
+        kw = {}
+        if bias is not None:
+            kw["bias"] = ap(bias)
+        if scale is not None:
+            kw["scale"] = ap(scale)
+        if accum is not None:
+            kw["accum_out"] = accum[0]
+        emit("a", lambda: g.scalar.activation(out[0], in_[0], func, **kw), rd(in_, bias, scale),
+             out[1] + (accum[1] if accum is not None else []))
+
+    def mm(out, w, ws, x, xs):
+        emit("t", lambda: g.tensor.matmul_mx(out[0], w[0], ws[0], x[0], xs[0], True, True), rd(w, ws, x, xs), out[1])
+
+    def iota(out, pattern, base, cm, flag=False):
+        kw = {"allow_small_or_imprecise_dtypes": True} if flag else {}
+        emit("p", lambda: g.iota(out[0], pattern, base, cm, **kw), [], out[1])
+
+    (kI, kNI, kM0, kM5, kML, kG0, kG1, kG2, kL0, kL1, kL2, kCA, kCA0, kCB, kCB0, kI48, kT) = [
+        A("col", k, k + 1) for k in range(17)]
+    md, r16 = lambda n: A("md", 0, n), lambda n: A("r16", 0, n)
+
+    dma("s", A("ut", 0, 512), ext(T.u[:, :]))
+    dma("a", A("x0", 0, 768), ext(T.x[:, 0:768]))
+    dma("s", A("x0", 768, 1536), ext(T.x[:, 768:1536]))
+    dma("a", A("nbl", 0, 48), ext(T.nb[:, :]))
+    rows = [("nbw%d" % i, 0, 768, 1) for i in range(16)]
+    for i in range(16):
+        dma("sa"[i % 2], (T.nbw[i:128:16, :], [rows[i]]), ext(T.nb[:, :]))
+    nbw = (T.nbw[:, 0:768], rows)
+    dma("s", U8("qw", 0, 512), ext(T.wc[:, :]))
+    dma("s", A("sw", 0, 512), ext(T.ws[:, :]))
+    dma("s", A("vt", 0, 512), ext(T.v[:, :]))
+
+    iota(A("pi", 0, 1), [[1, 1]], 0, 1)
+    iota(A("li5", 0, 8), [[16, 8]], 0, 0)
+    iota(A("li2", 0, 24), [[16, 24]], 0, 0)
+    iota(A("li", 0, 48), [[1, 48]], 0, 0)
+    iota(A("jm16", 0, 768), [[0, 48], [1, 16]], 0, 0, True)
+    iota(A("idr", 0, C), [[1, C]], 0, 0, True)
+    iota(A("li3", 0, 20), [[1, 5], [16, 4]], 0, 0)
+    iota(A("li4", 0, 24), [[NB, 24]], NB - 1, 0)
+    for b in range(4):
+        iota(A("db%d" % b, C, C + 16), [[0, 16]], 0, 0, True)
+    iota(A("ones", 0, 512), [[0, 512]], 1, 0, True)
+    for b in range(4):
+        out, one = A("et", 512 * b, 512 * b + 512), A("ones", 0, 512)
+        emit("p", lambda: g.affine_select(out[0], one[0], [[4, 128], [1, 4]], O.is_equal, 0.0, -b, -4), one[1], out[1])
+    for b in range(4):
+        iota(A("hs%d" % b, SL, SL + 8), [[0, 8]], 0, 0, True)
+    iota(A("one6", 0, 6 * EB), [[0, 6 * EB]], 1, 0, True)
+    ts(A("pi", 1, 2), A("pi", 0, 1), 15, O.bitwise_and)
+    tc(A("upl", 0, 8), A("li5", 0, 8))
+    ts(kI, A("pi", 1, 2), 1.0, O.mult)
+    ts(kNI, A("pi", 1, 2), -1.0, O.mult)
+    ts(kM0, kI, 0.0, O.is_equal)
+    ts(kM5, kI, 5.0, O.is_equal)
+    ts(kT, kI, 4.0, O.is_le)
+    ts(kI48, kI, 48.0, O.mult)
+    act(A("jz", 0, 768), A("jm16", 0, 768), AF.Square, bias=kNI)
+    act(md(768), A("jz", 0, 768), AF.Relu, bias=1.0, scale=-1.0)
+    act(r16(768), A("jm16", 0, 768), AF.Sign)
+    act(A("lx", 0, C), A("idr", 0, C), scale=kM0)
+    act(A("lx", C, 2 * C), A("idr", 0, C), scale=kM0)
+    ts(kCA, kI, 16.0, O.mult, 1.0, O.add)
+    ts(kCB, kI, 1.0, O.add)
+    tt(kML, kM0, kM5, O.add)
+    for k, (a, b) in enumerate(((kG0, kL0), (kG1, kL1), (kG2, kL2))):
+        ts(a, kI, float(k + 2), O.is_ge, kT, O.mult)
+    ts(A("inl", 0, 48), A("li", 0, 48), kI48, O.add)
+    ts(A("nl", 0, 24), A("li2", 0, 24), kI, O.add)
+    for a, b in ((kML, kML), (kG0, kL0), (kG1, kL1), (kG2, kL2)):
+        ts(b, a, -1.0, O.mult, 1.0, O.add)
+    ts(kCA0, kM0, -2.0, O.mult, kCA, O.add)
+    ts(kCB0, kM0, -2.0, O.mult, kCB, O.add)
+    quant(A("qu0", 0, 128), A("su0", 0, 128), A("ut", 0, 512))
+    tc(U32("qu", 0, 128), I(U32("qu0", 0, 128), A("upl", 0, 8)))
+    tc(A("su", 0, 128), I(A("su0", 0, 128), A("upl", 0, 8)))
+
+    qx, sx, S = A("qx", 0, C), A("sx", 0, C), A("pS", 0, C)
+
+    def scores(t):
+        quant(qx, sx, A("x%d" % t, 0, 4 * C))
+        mm(S, A("qu", 0, 128), A("su", 0, 128), qx, sx)
+
+    scores(0)
+    tc(A("lrep", 0, 768), I(nbw, A("inl", 0, 48)))
+    tc(A("lu", 0, 48), A("nbl", 0, 48))
+    tc(A("ll", 0, 48), A("nbl", 0, 48))
+    act(A("lsn", 0, 768), A("lrep", 0, 768), scale=kML)
+    tt(A("dl", 0, 24), A("ll", 24, 48), A("ll", 0, 24), O.subtract)
+
+    def late_constants():
+        quant(A("qe", 0, 512), A("se", 0, 512), A("et", 0, 2048))
+        tc(A("exr", 0, 24), A("li4", 0, 24))
+        tc(A("exp", 0, 20), A("li3", 0, 20))
+        f = [16 * i + j + 1 for _, i, j in PAIRS]
+        f[0] = 0
+        steps = [float(-f[-1])] + [float(f[r] - f[r - 1]) for r in range(len(PAIRS) - 1, 0, -1)] + [0.0, 0.0]
+        for e in range(NB):
+            fill(A("d1k", e, 24 * NB, NB), steps[e])
+        fill(A("ne", 0, 24 * NB, NB), 0.0)
+        act(A("mk", 0, C), md(C), AF.Identity, bias=-2e29, scale=5e29)
+        act(A("d0f", 0, C), r16(C), AF.Identity, bias=-2e29, scale=5e29)
+        act(A("r16b", 0, C), r16(C))
+
+    def last_constants():
+        for out, back in (("pz", False), ("px", True)):
+            if back:
+                ts(A("ce", 0, 20), A("nl", 0, 20), -1.0, O.mult, float(SL - 1), O.add)
+            else:
+                tc(A("ce", 0, 20), A("nl", 0, 20))
+            ts(A("ca", 0, 20), A("ce", 0, 20), 205.0, O.mult)
+            ts(A("cb", 0, 20), A("ca", 0, 20), 10, O.arith_shift_right)
+            ts(A("cc", 0, 20), A("cb", 0, 20), -319.0, O.mult)
+            ts(A("cd", 0, 20), A("ce", 0, 20), 64.0, O.mult)
+            tt(A("ce", 0, 20), A("cc", 0, 20), A("cd", 0, 20), O.add)
+            tc(A(out, 0, 20), A("ce", 0, 20))
+
+    def search_constants():
+        ts(A("nm", 0, 24), A("nl", 0, 24), -192.0, O.add)
+        ts(A("nbias", 0, 24), A("nl", 0, 24), -32.0, O.mult, 32.0 * 192, O.add)
+        fill(A("d0e", 0, 24 * EB, EB), 0.0)
+        fill(A("d0e", 1, 24 * EB, EB), 0.0)
+        quant(A("qv", 0, 128), A("sv", 0, 128), A("vt", 0, 512))
+
+    for t in range(R):
+        last = t == R - 1
+        if t:
+            scores(t)
+        tt(A("smd", 0, C), S, md(C), O.mult)
+        act(A("sm5", 0, C), S, scale=kM5)
+        scan(A("sn", 0, C), r16(C), A("smd", 0, C), O.mult, O.add)
+        sl = A("sn", 15, C, 16)
+        ts(A("fl", 0, 24), sl, 0.0, O.is_gt)
+        ts(A("fx", 0, 24), sl, 0.0, O.is_gt, 384.0, O.mult)
+        tt(A("cm", 0, 24), A("fl", 0, 24), A("dl", 0, 24), O.mult)
+        tt(A("ix", 0, 24), A("fx", 0, 24), A("nl", 0, 24), O.add)
+        tt(A("cl", 0, 24), A("cm", 0, 24), A("ll", 0, 24), O.add)
+        tc(A("ixu", 0, 24), A("ix", 0, 24))
+        tc(A("cu", 0, 24), A("cl", 0, 24))
+        if t == 0:
+            tt(A("ltyp", 0, 768), A("lsn", 0, 768), A("lx", 0, 768), O.add)
+        tt(A("v0", 0, C), I(A("ltyp", 0, 768), A("ixu", 0, 24)), A("sm5", 0, C), O.add)
+        for k, (up, stay) in enumerate(((kG0, kL0), (kG1, kL1), (kG2, kL2))):
+            act(A("vb", 0, C), A("v%d" % k, 0, C), scale=stay)
+            ts(A("va", 0, C), A("v%d" % k, 0, C), up, O.mult)
+            tt(A("v%d" % (k + 1), 0, C), I(A("va", 0, C), A("cu", 0, 24)), A("vb", 0, C), O.add)
+        act(A("gg", 0, C), I(A("v3", 0, C), A("lu", 0, 24)))
+        tc(A("gg", C, 2 * C), I(A("v3", 0, C), A("lu", 24, 48)))
+        if t == 0:
+            late_constants()
+        for b in range(4):
+            mm(A("pF%d" % b, 0, C), A("qe", 128 * b, 128 * b + 128), A("se", 128 * b, 128 * b + 128), qx, sx)
+        turn(A("gt", C, 2 * C), A("gg", C, 2 * C))
+        turn(A("gt", 0, C), A("gg", 0, C))
+        for b in range(4):
+            act(A("fb%d" % b, 0, C), A("pF%d" % b, 0, C))
+            act(A("db%d" % b, 0, C), A("pF%d" % b, 0, C), scale=0.5)
+        p = lambda i: A("gt", i, C, 16)
+        q = lambda j: A("gt", C + j, 2 * C, 16)
+        tt(A("ow", 0, 24), q(5), p(5), O.is_gt)
+        for r in range(1, len(PAIRS)):
+            tt(A("ne", 25 - r, 24 * NB, NB), p(PAIRS[r][1]), q(PAIRS[r][2]), O.not_equal)
+        tt(A("ne", 25, 24 * NB, NB), p(0), q(0), O.not_equal)
+        ts(A("ne", 26, 24 * NB, NB), A("ow", 0, 24), -2.0, O.mult, 1.0, O.add)
+        scan(A("st", 0, 24 * NB), A("ne", 0, 24 * NB), A("d1k", 0, 24 * NB), O.mult, O.add)
+        tc(A("ex", 0, C), I(A("st", 0, 24 * NB), A("exr", 0, 24)))
+        turn(A("kr", 0, C), A("ex", 0, C))
+        act(A("ka", 0, C), A("kr", 0, C), AF.Abs)
+        ts(A("tm", 0, C), A("kr", 0, C), 0.0, O.is_equal, -BIG, O.mult)
+        tt(A("ms", 0, C), S, A("tm", 0, C), O.add)
+        tt(A("mi", 0, C), A("ms", 0, C), A("mk", 0, C), O.min)
+        scan(A("ff", 0, C), A("d0f", 0, C), A("mi", 0, C), O.min, O.max)
+        for c in range(24):
+            s, m0, e, j0 = A("ff", 16 * c + 15, 16 * c + 16), C * (c % 6), 16 * c + 16, C * (c % 4)
+            ts(A("mm", m0, m0 + e), A("ms", 0, e), s, O.is_lt)
+            if e < C:
+                ts(A("mm", m0 + e, m0 + C), A("ms", e, C), s, O.is_le)
+            act(A("junk", j0, j0 + C), A("mm", m0, m0 + C), accum=A("cnt", c, c + 1))
+        tt(A("eq", 0, C), A("ff", 0, C), A("ms", 0, C), O.is_equal)
+        scan(A("eqs", 0, C), A("r16b", 0, C), A("eq", 0, C), O.mult, O.add)
+        if t == 0:
+            last_constants()
+        tt(A("rk", 0, 24), A("cnt", 0, 24), A("eqs", 15, C, 16), O.add)
+        ts(A("rku", 0, 24), A("rk", 0, 24), -1.0, O.mult, 384.0, O.add)
+        scatter(A("order", 0, C), A("rku", 0, 24), A("idr", 0, C))
+        tt(A("o1", 0, 64), A("order", 0, 64), md(64), O.mult)
+        scan(A("ol", 0, 64), r16(64), A("o1", 0, 64), O.mult, O.add)
+        tc(A("ou", 0, 4), A("ol", 15, 64, 16))
+        ou = A("ou", 0, 4)
+        tc(A("kai", 0, 64), I(A("ka", 0, C), ou))
+        tc(A("km", 0, 64), I(A("kr", 0, C), ou))
+        tc(A("pm", 0, 64), I(A("gg", 0, C), ou))
+        tc(A("qm", 0, 64), I(A("gg", C, 2 * C), ou))
+        ts(A("jm", 0, 64), A("kai", 0, 64), 15, O.bitwise_and)
+        ts(A("ht", 0, 64), A("kai", 0, 64), kCA0, O.is_lt)
+        ts(A("pab", 0, 64), A("kai", 0, 64), kCA, O.is_ge)
+        ts(A("ht", 64, 128), A("jm", 0, 64), kCB0, O.is_lt)
+        ts(A("pab", 64, 128), A("jm", 0, 64), kCB, O.is_ge)
+        ts(A("ht", 256, 320), A("km", 0, 64), 0.0, O.is_lt, -511.0, O.mult)
+        ts(A("ht", 320, 384), A("kai", 0, 64), 0.0, O.is_equal, float(C * 513), O.mult)
+        tt(A("ht", 128, 192), A("pab", 0, 64), A("pm", 0, 64), O.mult)
+        tt(A("ht", 192, 256), A("pab", 64, 128), A("qm", 0, 64), O.mult)
+        turn(A("htt", 0, 384), A("ht", 0, 384))
+        scan(A("ab", 0, 128), A("htt", 0, 128), A("htt", 128, 256), O.mult, O.add)
+        W = lambda k: A("w", 64 * k, 64 * k + 64)
+        tt(W(0), A("ab", 64, 128), A("ab", 0, 64), O.subtract)
+        ts(W(1), A("ab", 64, 128), 512.0, O.mult)
+        tt(W(2), A("ab", 0, 64), A("htt", 320, 384), O.add)
+        tt(W(3), W(0), A("htt", 256, 320), O.mult)
+        tt(W(4), W(1), W(2), O.add)
+        tt(A("pp", 0, 64), W(4), W(3), O.add)
+        tc(A("pe", 0, SL), I(A("pp", 0, 64), A("exp", 0, 20)))
+        turn(A("pr", 0, SL), A("pe", 0, SL))
+        tt(A("pl", 0, SL), I(A("pr", 0, SL), A("pz", 0, 20)), md(SL), O.mult)
+        scan(A("ps", 0, SL), r16(SL), A("pl", 0, SL), O.mult, O.add)
+        tc(A("pi3", 0, 20), A("ps", 15, SL, 16))
+        ts(A("pi3", 20, 40), A("pi3", 0, 20), 511, O.bitwise_and)
+        ts(A("pi3", 40, 60), A("pi3", 0, 20), 9, O.arith_shift_right)
+        tc(A("xyu", 0, 20), A("pi3", 20, 40))
+        tc(A("xyu", 20, 40), A("pi3", 40, 60))
+        for h in range(2):
+            for b in range(4):
+                z = A("za", HALF * (4 * h + b), HALF * (4 * h + b + 1))
+                win = A("db%d" % b, 0, C + 16)
+                act(z, I(win, A("xyu", 10 * h, 10 * h + 10)))
+                tt(A("zt%d" % h, b, 4 * HALF, 4), I(win, A("xyu", 20 + 10 * h, 30 + 10 * h)), z, O.add)
+            a, e = HALF * h, HALF * h + HALF
+            quant(A("zc%d" % t, a, e), A("zs%d" % t, a, e), A("zt%d" % h, 0, 4 * HALF))
+            order("p", [("zc%d" % t, a, e, 1), ("zs%d" % t, a, e, 1)], [])
+            g.remote_dma(T["lc%d" % t][:, a:e].bitcast(dt.uint8), T["zc%d" % t][:, a:e].bitcast(dt.uint8),
+                         T.sem["ar%d" % t], T.sem.lsent, pid, rid, mask)
+            g.remote_dma(T["ls%d" % t][:, a:e], T["zs%d" % t][:, a:e],
+                         T.sem["ar%d" % t], T.sem.lsent, pid, rid, mask)
+        note("ar%d" % t, 4 * width, [], [("lc%d" % t, 0, SL, 1), ("ls%d" % t, 0, SL, 1)])
+        if t == 0:
+            search_constants()
+        tc(A("pri", 0, SL), A("pr", 0, SL))
+        ts(A("xri", 0, SL), A("pri", 0, SL), 511, O.bitwise_and)
+        ts(A("xp", 0, SL), I(A("xri", 0, SL), A("px", 0, 20)), -192.0, O.add)
+        for c in list(range(VROWS, 24)) + list(range(VROWS)):
+            row = A("d0e", EB * c + 2, EB * c + EB)
+            if c < VROWS:
+                ts(row, A("xp", 0, SL), A("nm", c, c + 1), O.not_equal, 1024.0, O.mult)
+            else:
+                act(row, A("xp", 0, SL), AF.Square, bias=A("nbias", c, c + 1), scale=32.0)
+        tt(A("k1", 0, 64), A("km", 0, 64), md(64), O.mult)
+        n64 = lambda k: A("n64", 64 * k, 64 * k + 64)
+        ts(n64(0), A("kai", 0, 64), 0.0, O.is_gt)
+        scan(A("kl", 0, 64), r16(64), A("k1", 0, 64), O.mult, O.add)
+        if not last:
+            ts(A("tv", 0, 64), A("order", 0, 64), kM0, O.mult)
+        ts(A("po", 0, 4), A("kl", 15, 64, 16), 0.0, O.is_ge, 384.0, O.mult)
+        tt(A("po", 4, 8), A("po", 0, 4), A("ol", 15, 64, 16), O.add)
+        pu = A("pu", 0, 4)
+        tc(pu, A("po", 4, 8))
+        tc(n64(1), I(A("lrep", 0, 768), pu))
+        tt(n64(2), A("xri", 4 * M, 5 * M), n64(1), O.subtract)
+        tt(n64(3), n64(2), n64(0), O.mult)
+        tt(n64(4), n64(3), n64(1), O.add)
+        scatter(A("lrep", 0, 768), pu, n64(4))
+        if last:
+            dma("s", ext(T.ol[:, :]), (T.lrep[0:128:16, :], [("lrep", 0, 768, 1)]))
+        else:
+            ts(A("tv", 64, 128), n64(4), kML, O.mult)
+            tt(A("lx", 0, 768), A("lrep", 0, 768), md(768), O.mult)
+            tt(A("tv", 128, 192), A("tv", 64, 128), A("tv", 0, 64), O.add)
+            scan(A("lsn", 0, 768), r16(768), A("lx", 0, 768), O.mult, O.add)
+            scatter(A("ltyp", 0, 768), pu, A("tv", 128, 192))
+            tc(A("ll", 0, 48), A("lsn", 15, 768, 16))
+            tc(A("lu", 0, 48), A("lsn", 15, 768, 16))
+            tt(A("dl", 0, 24), A("ll", 24, 48), A("ll", 0, 24), O.subtract)
+        for k in range(4):
+            a, e = 6 * EB * k, 6 * EB * k + 6 * EB
+            scan(A("ste", a, e), A("d0e", a, e), A("one6", 0, 6 * EB), O.min, O.add)
+        ts(A("eu", 0, 24), A("ste", EB - 1, 24 * EB, EB), -1.0, O.add)
+        for b in range(4):
+            mm(A("pF%d" % b, 0, SL), A("qw", 128 * b, 128 * b + 128), A("sw", 128 * b, 128 * b + 128),
+               A("lc%d" % t, 0, SL), A("ls%d" % t, 0, SL))
+        for b in range(4):
+            act(A("hs%d" % b, 0, SL), A("pF%d" % b, 0, SL), scale=0.03125)
+            tt(A("x%d" % (t + 1), b, 4 * C, 4), I(A("hs%d" % b, 0, SL + 8), A("eu", 0, 24)), A("fb%d" % b, 0, C), O.add)
+
+    quant(qx, sx, A("x%d" % R, 0, 4 * C))
+    mm(S, A("qv", 0, 128), A("sv", 0, 128), qx, sx)
+    dma("s", ext(T.oc[:, :]), U8("qx", 0, C))
+    for k in range(4):
+        dma("as"[k % 2], ext(T.osc[4 * k:4 * k + 4, :]), (T.sx[32 * k:32 * k + 4, 0:C], sx[1]))
+    act(A("ys", 0, C), S)
+    dma("a", ext(T.y[:, :]), A("ys", 0, C))
+    for src in sorted(count):
+        need("p", src, count[src])
+    g.wait_ge(T.sem.lsent, R * 4 * width)
+    for t in range(R):
+        need("p", "ar%d" % t, 4 * width)

@@ -4,10 +4,15 @@ N, C, L, M, R = 4, 384, 5, 64, 3
 SL = L * M
 HALF = SL // 2
 PAIRS = sorted(((i + j, i, j) for i in range(L) for j in range(L)))
-NB = len(PAIRS) + 2
+NB = len(PAIRS) + 1
 EB = SL + 2
 BIG = 1e29
-VROWS = 4
+UP = 1024.0
+CUT = 224
+VROWS = 8
+AROWS = (20, 19)
+TILES = [(rows, max(128, 16 * min(max(rows), 24))) for rows in ([24, 23, 22, 21], [20, 19, 18, 17], [16, 15, 14, 13],
+                                                              [12, 11, 10, 9], [8, 7, 6, 5], [4, 3, 2, 1])]
 
 F32, BF, I32, U16, F16, COD = "float32", "bfloat16", "int32", "uint16", "float16", "float8_e4m3fn_x4"
 SCRATCH, PLACE = {}, {}
@@ -29,25 +34,26 @@ def _pool(pool, dtype, spec):
 
 
 _own(BF, "x0:1536 x1:1536 x2:1536 x3:1536 ut:512 vt:512 et:2048 ones:512 za:1280 zt0:640 zt1:640")
-_own(BF, "fb0:384 fb1:384 fb2:384 fb3:384 db0:400 db1:400 db2:400 db3:400")
+_own(BF, "fb0:384 fb1:384 fb2:384 fb3:384 db0:400 db1:400 db2:400 db3:400 bd:512 bd1:512 mt:5632")
 _own(F32, "hs0:328 hs1:328 hs2:328 hs3:328 lrep:768 ys:384")
 _own(I32, "nbl:48 nbw:768")
-for _n, _k in (("w", 512), ("v", 128), ("u0", 128), ("u", 128), ("e", 512), ("x", 384)):
+for _n, _k in (("w", 512), ("v", 128), ("u0", 128), ("u", 128), ("e", 512), ("x", 384), ("bd", 128), ("m", 1408)):
     _own(COD, "q%s:%d" % (_n, _k))
     _own("uint8", "s%s:%d" % (_n, _k))
 for _t in range(R):
     _own(COD, "zc%d:320 lc%d:320" % (_t, _t))
     _own("uint8", "zs%d:320 ls%d:320" % (_t, _t))
-_pool("poolf", F32, "jm16:768 jz:768 md:768 r16:768 mk:384 d0f:384 idr:384 col:32 nl:24 nm:24 nbias:24 cc:20 cd:20 ce:20 "
-      "ltyp:768 ll:48 dl:24 lx:768 lsn:768 smd:384 sn:384 sm5:384 fl:24 fx:24 ix:24 cm:24 cl:24 v0:384 v1:384 v2:384 "
-      "v3:384 va:384 vb:384 gg:768 gt:768 ow:24 ms:384 mi:384 ff:384 cnt:24 rk:24 order:384 o1:64 ol:64 pm:64 qm:64 "
-      "km:64 pab:128 ht:384 htt:384 ab:128 w:320 pp:64 pe:320 pr:320 pl:320 ps:320 k1:64 kl:64 po:8 n64:320 tv:192")
-_pool("poolb", BF, "r16b:384 d1k:648 one6:1932 ne:648 st:648 ex:384 kr:384 ka:384 tm:384 eq:384 eqs:384 mm:2304 "
+_pool("poolf", F32, "jm16:768 jz:768 jy:768 md:384 r16:384 da:768 db:768 mk:384 d0f:384 idr:384 b0:384 col:32 nl:24 nm:24 "
+      "nbias:24 cc:40 cd:40 ce:40 ll:48 l2:48 dl:24 la:768 lb:768 smd:384 sn:384 ssb:384 sp:768 fl:24 fx:24 ix:24 cm:24 "
+      "cl:24 v0:384 v1:384 v2:384 v3:384 vb:384 npos:24 rk2:24 cx:384 cs:384 ms:384 mi:384 ff:384 cnt:24 rk:24 order:384 "
+      "o1:64 ol:64 pm:64 qn:64 sc:128 on:64 pab:128 ht:384 htt:384 ab:128 w:320 pp:64 pe:320 pr:320 pl:320 ps:320 k1:64 "
+      "kl:64 po:8 n64:320")
+_pool("poolb", BF, "gg:768 gt:768 r16b:384 d1k:624 one6:1932 ne:624 st:624 ex:384 kr:384 tm:384 sg:1536 eqs:384 "
       "junk:1536 xp:320 d0e:7728")
-_pool("pooli", I32, "pi:2 li:48 li2:24 li3:20 li4:24 li5:8 ca:20 cb:20 kai:64 jm:64 pi3:60 pri:320 xri:320")
-_pool("poolu", U16, "upl:8 inl:48 exr:24 exp:20 pz:20 px:20 lu:48 ixu:24 cu:24 rku:24 ou:4 xyu:40 eu:24 pu:4")
+_pool("pooli", I32, "pi:2 li:48 li2:24 li3:20 li4:24 li5:8 ca:40 cb:40 kai:64 jm:64 pi3:60 pri:320 xri:320")
+_pool("poolu", U16, "upl:8 inl:48 exr:24 exp:20 pz:40 lu:48 ixu:24 cu:24 rku:24 ou:4 xyu:40 eu:24 pu:4")
 _pool("poolh", F16, "ste:7728")
-PSUM = ("pS", "pF0", "pF1", "pF2", "pF3")
+PSUM = ("pS", "pC", "pF0", "pF1", "pF2", "pF3")
 for _n in PSUM:
     SCRATCH[_n] = ("psum", [128, 512], F32)
 NDMA = 40
@@ -180,14 +186,20 @@ def rank_program(g, core, T, topo):
         emit("a", lambda: g.scalar.activation(out[0], in_[0], func, **kw), rd(in_, bias, scale),
              out[1] + (accum[1] if accum is not None else []))
 
-    def mm(out, w, ws, x, xs):
-        emit("t", lambda: g.tensor.matmul_mx(out[0], w[0], ws[0], x[0], xs[0], True, True), rd(w, ws, x, xs), out[1])
+    def mm(out, w, ws, x, xs, start=True, stop=True):
+        emit("t", lambda: g.tensor.matmul_mx(out[0], w[0], ws[0], x[0], xs[0], start, stop), rd(w, ws, x, xs),
+             out[1] if start else [])
+        if not start:
+            note(semof["t"], count[semof["t"]], [], [("pC", 0, C, 1)])
 
     def iota(out, pattern, base, cm, flag=False):
         kw = {"allow_small_or_imprecise_dtypes": True} if flag else {}
         emit("p", lambda: g.iota(out[0], pattern, base, cm, **kw), [], out[1])
 
-    (kI, kNI, kM0, kM5, kML, kG0, kG1, kG2, kL0, kL1, kL2, kCA, kCA0, kCB, kCB0, kI48, kT) = [
+    def choose(out, in_, pattern, cmp, base, cm):
+        emit("p", lambda: g.affine_select(out[0], in_[0], pattern, cmp, 0.0, base, cm), in_[1], out[1])
+
+    (kI, kM0, kMU, kL0, kL1, kL2, kU0, kU1, kU2, kOff, kCA, kCA0, kCB, kCB0, kI48, kT, knot15) = [
         A("col", k, k + 1) for k in range(17)]
     md, r16 = lambda n: A("md", 0, n), lambda n: A("r16", 0, n)
 
@@ -213,37 +225,36 @@ def rank_program(g, core, T, topo):
     iota(A("li4", 0, 24), [[NB, 24]], NB - 1, 0)
     for b in range(4):
         iota(A("db%d" % b, C, C + 16), [[0, 16]], 0, 0, True)
-    iota(A("ones", 0, 512), [[0, 512]], 1, 0, True)
+    ones, half, blocks = A("ones", 0, 512), A("bd1", 0, 512), A("bd", 0, 512)
+    iota(ones, [[0, 512]], 1, 0, True)
     for b in range(4):
-        out, one = A("et", 512 * b, 512 * b + 512), A("ones", 0, 512)
-        emit("p", lambda: g.affine_select(out[0], one[0], [[4, 128], [1, 4]], O.is_equal, 0.0, -b, -4), one[1], out[1])
+        choose(A("et", 512 * b, 512 * b + 512), ones, [[4, 128], [1, 4]], O.is_equal, -b, -4)
+    choose(half, ones, [[-16, 8], [0, 64]], O.is_ge, 0, 1)
+    choose(blocks, half, [[16, 8], [0, 64]], O.is_ge, 15, -1)
     for b in range(4):
         iota(A("hs%d" % b, SL, SL + 8), [[0, 8]], 0, 0, True)
     iota(A("one6", 0, 6 * EB), [[0, 6 * EB]], 1, 0, True)
     ts(A("pi", 1, 2), A("pi", 0, 1), 15, O.bitwise_and)
     tc(A("upl", 0, 8), A("li5", 0, 8))
-    ts(kI, A("pi", 1, 2), 1.0, O.mult)
-    ts(kNI, A("pi", 1, 2), -1.0, O.mult)
+    tc(kI, A("pi", 1, 2))
     ts(kM0, kI, 0.0, O.is_equal)
-    ts(kM5, kI, 5.0, O.is_equal)
-    ts(kT, kI, 4.0, O.is_le)
-    ts(kI48, kI, 48.0, O.mult)
-    act(A("jz", 0, 768), A("jm16", 0, 768), AF.Square, bias=kNI)
-    act(md(768), A("jz", 0, 768), AF.Relu, bias=1.0, scale=-1.0)
-    act(r16(768), A("jm16", 0, 768), AF.Sign)
-    act(A("lx", 0, C), A("idr", 0, C), scale=kM0)
-    act(A("lx", C, 2 * C), A("idr", 0, C), scale=kM0)
-    ts(kCA, kI, 16.0, O.mult, 1.0, O.add)
     ts(kCB, kI, 1.0, O.add)
-    tt(kML, kM0, kM5, O.add)
-    for k, (a, b) in enumerate(((kG0, kL0), (kG1, kL1), (kG2, kL2))):
-        ts(a, kI, float(k + 2), O.is_ge, kT, O.mult)
+    ts(kI48, kI, 48.0, O.mult)
+    ts(kMU, kI, 0.0, O.is_equal, UP, O.mult)
+    act(A("jz", 0, C), A("jm16", 0, C), AF.Square, bias=kI, scale=-1.0)
+    act(md(C), A("jz", 0, C), AF.Relu, bias=1.0, scale=-1.0)
+    act(r16(C), A("jm16", 0, C), AF.Sign)
+    act(A("b0", 0, C), A("idr", 0, C), AF.Identity, bias=kMU, scale=kM0)
     ts(A("inl", 0, 48), A("li", 0, 48), kI48, O.add)
     ts(A("nl", 0, 24), A("li2", 0, 24), kI, O.add)
-    for a, b in ((kML, kML), (kG0, kL0), (kG1, kL1), (kG2, kL2)):
-        ts(b, a, -1.0, O.mult, 1.0, O.add)
-    ts(kCA0, kM0, -2.0, O.mult, kCA, O.add)
+    for k, (stay, up) in enumerate(((kL0, kU0), (kL1, kU1), (kL2, kU2))):
+        ts(stay, kI, k + 1.5, O.is_lt)
+        ts(up, kI, k + 1.5, O.is_lt, UP, O.mult)
+    ts(kT, kI, UP, O.mult, -4 * UP, O.add)
+    ts(kCA, kI, 16.0, O.mult, 1.0, O.add)
     ts(kCB0, kM0, -2.0, O.mult, kCB, O.add)
+    ts(kOff, kT, 0.0, O.min, -192.0, O.add)
+    ts(kCA0, kM0, -2.0, O.mult, kCA, O.add)
     quant(A("qu0", 0, 128), A("su0", 0, 128), A("ut", 0, 512))
     tc(U32("qu", 0, 128), I(U32("qu0", 0, 128), A("upl", 0, 8)))
     tc(A("su", 0, 128), I(A("su0", 0, 128), A("upl", 0, 8)))
@@ -254,125 +265,155 @@ def rank_program(g, core, T, topo):
         quant(qx, sx, A("x%d" % t, 0, 4 * C))
         mm(S, A("qu", 0, 128), A("su", 0, 128), qx, sx)
 
-    scores(0)
-    tc(A("lrep", 0, 768), I(nbw, A("inl", 0, 48)))
-    tc(A("lu", 0, 48), A("nbl", 0, 48))
-    tc(A("ll", 0, 48), A("nbl", 0, 48))
-    act(A("lsn", 0, 768), A("lrep", 0, 768), scale=kML)
-    tt(A("dl", 0, 24), A("ll", 24, 48), A("ll", 0, 24), O.subtract)
-
     def late_constants():
         quant(A("qe", 0, 512), A("se", 0, 512), A("et", 0, 2048))
         tc(A("exr", 0, 24), A("li4", 0, 24))
         tc(A("exp", 0, 20), A("li3", 0, 20))
         f = [16 * i + j + 1 for _, i, j in PAIRS]
         f[0] = 0
-        steps = [float(-f[-1])] + [float(f[r] - f[r - 1]) for r in range(len(PAIRS) - 1, 0, -1)] + [0.0, 0.0]
+        steps = [-f[-1]] + [f[r] - f[r - 1] for r in range(len(PAIRS) - 1, 0, -1)] + [0]
+        most = max(steps, key=steps.count)
+        fill(A("d1k", 0, 24 * NB), float(most))
         for e in range(NB):
-            fill(A("d1k", e, 24 * NB, NB), steps[e])
+            if steps[e] != most:
+                fill(A("d1k", e, 24 * NB, NB), float(steps[e]))
         fill(A("ne", 0, 24 * NB, NB), 0.0)
+        quant(A("qbd", 0, 128), A("sbd", 0, 128), blocks)
+        fill(A("cnt", 0, 1), 0.0)
+        at = 0
+        for rows, w in TILES:
+            fill(A("mt", at + 64 * min(rows), at + 4 * w), 0.0)
+            at += 4 * w
+        ts(A("npos", 0, 24), A("li2", 0, 24), kI, O.subtract, 15.0, O.add)
+        ts(knot15, kI, 15.0, O.is_lt)
         act(A("mk", 0, C), md(C), AF.Identity, bias=-2e29, scale=5e29)
         act(A("d0f", 0, C), r16(C), AF.Identity, bias=-2e29, scale=5e29)
         act(A("r16b", 0, C), r16(C))
 
     def last_constants():
-        for out, back in (("pz", False), ("px", True)):
-            if back:
-                ts(A("ce", 0, 20), A("nl", 0, 20), -1.0, O.mult, float(SL - 1), O.add)
-            else:
-                tc(A("ce", 0, 20), A("nl", 0, 20))
-            ts(A("ca", 0, 20), A("ce", 0, 20), 205.0, O.mult)
-            ts(A("cb", 0, 20), A("ca", 0, 20), 10, O.arith_shift_right)
-            ts(A("cc", 0, 20), A("cb", 0, 20), -319.0, O.mult)
-            ts(A("cd", 0, 20), A("ce", 0, 20), 64.0, O.mult)
-            tt(A("ce", 0, 20), A("cc", 0, 20), A("cd", 0, 20), O.add)
-            tc(A(out, 0, 20), A("ce", 0, 20))
+        act(A("ce", 0, 20), A("nl", 0, 20))
+        act(A("ce", 20, 40), A("nl", 0, 20), AF.Identity, bias=float(SL - 1), scale=-1.0)
+        act(A("cd", 0, 40), A("ce", 0, 40), scale=64.0)
+        ts(A("ca", 0, 40), A("ce", 0, 40), 205.0, O.mult)
+        ts(A("cb", 0, 40), A("ca", 0, 40), 10, O.arith_shift_right)
+        ts(A("cc", 0, 40), A("cb", 0, 40), -319.0, O.mult)
+        tt(A("ce", 0, 40), A("cc", 0, 40), A("cd", 0, 40), O.add)
+        tc(A("pz", 0, 40), A("ce", 0, 40))
+        act(A("jz", 0, 768), A("jm16", 0, 768), AF.Square, bias=kI, scale=-1.0)
+        act(A("da", 0, 768), A("jz", 0, 768), AF.Sign)
+        act(A("jy", 0, 768), A("jm16", 0, 768), AF.Square, bias=kCB, scale=-1.0)
+        act(A("db", 0, 768), A("jy", 0, 768), AF.Sign)
 
     def search_constants():
-        ts(A("nm", 0, 24), A("nl", 0, 24), -192.0, O.add)
-        ts(A("nbias", 0, 24), A("nl", 0, 24), -32.0, O.mult, 32.0 * 192, O.add)
+        act(A("nm", 0, 24), A("nl", 0, 24), AF.Identity, bias=-192.0)
+        act(A("nbias", 0, 24), A("nl", 0, 24), AF.Identity, bias=32.0 * 192, scale=-32.0)
         fill(A("d0e", 0, 24 * EB, EB), 0.0)
         fill(A("d0e", 1, 24 * EB, EB), 0.0)
         quant(A("qv", 0, 128), A("sv", 0, 128), A("vt", 0, 512))
 
     for t in range(R):
         last = t == R - 1
-        if t:
-            scores(t)
+        scores(t)
+        if t == 0:
+            tc(A("lrep", 0, 768), I(nbw, A("inl", 0, 48)))
+            tc(A("ll", 0, 48), A("nbl", 0, 48))
+        else:
+            scan(A("la", 0, 768), A("da", 0, 768), A("lrep", 0, 768), O.mult, O.add)
+            scan(A("lb", 0, 768), A("db", 0, 768), A("lrep", 0, 768), O.mult, O.add)
+            ts(A("l2", 0, 48), A("lb", 15, 768, 16), knot15, O.mult)
+            tt(A("ll", 0, 48), A("la", 15, 768, 16), A("l2", 0, 48), O.subtract)
         tt(A("smd", 0, C), S, md(C), O.mult)
-        act(A("sm5", 0, C), S, scale=kM5)
+        act(A("ssb", 0, C), S)
+        tt(A("dl", 0, 24), A("ll", 24, 48), A("ll", 0, 24), O.subtract)
         scan(A("sn", 0, C), r16(C), A("smd", 0, C), O.mult, O.add)
         sl = A("sn", 15, C, 16)
-        ts(A("fl", 0, 24), sl, 0.0, O.is_gt)
         ts(A("fx", 0, 24), sl, 0.0, O.is_gt, 384.0, O.mult)
-        tt(A("cm", 0, 24), A("fl", 0, 24), A("dl", 0, 24), O.mult)
+        ts(A("fl", 0, 24), sl, 0.0, O.is_gt)
         tt(A("ix", 0, 24), A("fx", 0, 24), A("nl", 0, 24), O.add)
-        tt(A("cl", 0, 24), A("cm", 0, 24), A("ll", 0, 24), O.add)
+        tt(A("cm", 0, 24), A("fl", 0, 24), A("dl", 0, 24), O.mult)
         tc(A("ixu", 0, 24), A("ix", 0, 24))
+        tt(A("cl", 0, 24), A("cm", 0, 24), A("ll", 0, 24), O.add)
+        tt(A("v0", 0, C), I(A("lrep", 0, 768), A("ixu", 0, 24)), A("b0", 0, C), O.max)
         tc(A("cu", 0, 24), A("cl", 0, 24))
-        if t == 0:
-            tt(A("ltyp", 0, 768), A("lsn", 0, 768), A("lx", 0, 768), O.add)
-        tt(A("v0", 0, C), I(A("ltyp", 0, 768), A("ixu", 0, 24)), A("sm5", 0, C), O.add)
-        for k, (up, stay) in enumerate(((kG0, kL0), (kG1, kL1), (kG2, kL2))):
-            act(A("vb", 0, C), A("v%d" % k, 0, C), scale=stay)
-            ts(A("va", 0, C), A("v%d" % k, 0, C), up, O.mult)
-            tt(A("v%d" % (k + 1), 0, C), I(A("va", 0, C), A("cu", 0, 24)), A("vb", 0, C), O.add)
-        act(A("gg", 0, C), I(A("v3", 0, C), A("lu", 0, 24)))
-        tc(A("gg", C, 2 * C), I(A("v3", 0, C), A("lu", 24, 48)))
+        tc(A("lu", 0, 48), A("ll", 0, 48))
+        for k, (stay, up) in enumerate(((kL0, kU0), (kL1, kU1), (kL2, kU2))):
+            act(A("vb", 0, CUT), A("v%d" % k, 0, CUT), AF.Identity, bias=up, scale=stay)
+            ts(A("vb", CUT, C), A("v%d" % k, CUT, C), stay, O.mult, up, O.add)
+            tt(A("v%d" % (k + 1), 0, C), I(A("v%d" % k, 0, C), A("cu", 0, 24)), A("vb", 0, C), O.max)
+        act(A("gg", 0, C), I(A("v3", 0, C), A("lu", 0, 24)), AF.Identity, bias=kOff)
+        ts(A("gg", C, 2 * C), I(A("v3", 0, C), A("lu", 24, 48)), kOff, O.add)
         if t == 0:
             late_constants()
         for b in range(4):
             mm(A("pF%d" % b, 0, C), A("qe", 128 * b, 128 * b + 128), A("se", 128 * b, 128 * b + 128), qx, sx)
         turn(A("gt", C, 2 * C), A("gg", C, 2 * C))
         turn(A("gt", 0, C), A("gg", 0, C))
+        act(A("sp", 0, 768), I(A("ssb", 0, C), A("lu", 0, 48)))
         for b in range(4):
             act(A("fb%d" % b, 0, C), A("pF%d" % b, 0, C))
             act(A("db%d" % b, 0, C), A("pF%d" % b, 0, C), scale=0.5)
         p = lambda i: A("gt", i, C, 16)
         q = lambda j: A("gt", C + j, 2 * C, 16)
-        tt(A("ow", 0, 24), q(5), p(5), O.is_gt)
-        for r in range(1, len(PAIRS)):
+        for r in range(len(PAIRS)):
             tt(A("ne", 25 - r, 24 * NB, NB), p(PAIRS[r][1]), q(PAIRS[r][2]), O.not_equal)
-        tt(A("ne", 25, 24 * NB, NB), p(0), q(0), O.not_equal)
-        ts(A("ne", 26, 24 * NB, NB), A("ow", 0, 24), -2.0, O.mult, 1.0, O.add)
         scan(A("st", 0, 24 * NB), A("ne", 0, 24 * NB), A("d1k", 0, 24 * NB), O.mult, O.add)
         tc(A("ex", 0, C), I(A("st", 0, 24 * NB), A("exr", 0, 24)))
         turn(A("kr", 0, C), A("ex", 0, C))
-        act(A("ka", 0, C), A("kr", 0, C), AF.Abs)
         ts(A("tm", 0, C), A("kr", 0, C), 0.0, O.is_equal, -BIG, O.mult)
         tt(A("ms", 0, C), S, A("tm", 0, C), O.add)
         tt(A("mi", 0, C), A("ms", 0, C), A("mk", 0, C), O.min)
         scan(A("ff", 0, C), A("d0f", 0, C), A("mi", 0, C), O.min, O.max)
-        for c in range(24):
-            s, m0, e, j0 = A("ff", 16 * c + 15, 16 * c + 16), C * (c % 6), 16 * c + 16, C * (c % 4)
-            ts(A("mm", m0, m0 + e), A("ms", 0, e), s, O.is_lt)
-            if e < C:
-                ts(A("mm", m0 + e, m0 + C), A("ms", e, C), s, O.is_le)
-            act(A("junk", j0, j0 + C), A("mm", m0, m0 + C), accum=A("cnt", c, c + 1))
-        tt(A("eq", 0, C), A("ff", 0, C), A("ms", 0, C), O.is_equal)
-        scan(A("eqs", 0, C), A("r16b", 0, C), A("eq", 0, C), O.mult, O.add)
+        spot, at = {}, 0
+        for rows, w in TILES:
+            for i, c in enumerate(rows):
+                spot[c] = A("mt", at + i, at + 64 * min(c, 24), 4)
+            at += 4 * w
+        score = lambda c: A("ff", 16 * c + 15, 16 * c + 16)
+        for c in AROWS:
+            sg = A("sg", C * (c % 4), C * (c % 4) + 16 * c)
+            act(sg, A("ms", 0, 16 * c), AF.Sign, bias=score(c), scale=-1.0)
+            act(spot[c], sg, AF.Relu, accum=A("cnt", c, c + 1))
+        at = 0
+        for k, (rows, w) in enumerate(TILES):
+            for c in rows:
+                if c == 24:
+                    tt(spot[c], A("ms", 0, C), A("ff", 0, C), O.is_le)
+                    scan(A("eqs", 0, C), A("r16b", 0, C), spot[c], O.mult, O.add)
+                elif c not in AROWS:
+                    ts(spot[c], A("ms", 0, 16 * c), score(c), O.is_lt)
+                    act(A("junk", C * (c % 4), C * (c % 4) + 16 * c), spot[c], accum=A("cnt", c, c + 1))
+            a = at // 4
+            quant(A("qm", a, a + w), A("sm", a, a + w), A("mt", at, at + 4 * w))
+            mm(A("pC", 0, w), A("qbd", 0, 128), A("sbd", 0, 128), A("qm", a, a + w), A("sm", a, a + w), k == 0, k == 5)
+            at += 4 * w
         if t == 0:
             last_constants()
-        tt(A("rk", 0, 24), A("cnt", 0, 24), A("eqs", 15, C, 16), O.add)
-        ts(A("rku", 0, 24), A("rk", 0, 24), -1.0, O.mult, 384.0, O.add)
+        tt(A("rk", 0, 24), A("npos", 0, 24), A("eqs", 15, C, 16), O.subtract)
+        tt(A("cx", 0, C), A("pC", 0, C), md(C), O.mult)
+        tt(A("rk2", 0, 24), A("rk", 0, 24), A("cnt", 0, 24), O.subtract)
+        scan(A("cs", 0, C), r16(C), A("cx", 0, C), O.mult, O.add)
+        tt(A("rk", 0, 24), A("rk2", 0, 24), A("cs", 15, C, 16), O.add)
+        tc(A("rku", 0, 24), A("rk", 0, 24))
         scatter(A("order", 0, C), A("rku", 0, 24), A("idr", 0, C))
         tt(A("o1", 0, 64), A("order", 0, 64), md(64), O.mult)
         scan(A("ol", 0, 64), r16(64), A("o1", 0, 64), O.mult, O.add)
         tc(A("ou", 0, 4), A("ol", 15, 64, 16))
         ou = A("ou", 0, 4)
-        tc(A("kai", 0, 64), I(A("ka", 0, C), ou))
-        tc(A("km", 0, 64), I(A("kr", 0, C), ou))
-        tc(A("pm", 0, 64), I(A("gg", 0, C), ou))
-        tc(A("qm", 0, 64), I(A("gg", C, 2 * C), ou))
+        for h in range(2):
+            act(A("sc", 64 * h, 64 * h + 64), I(A("sp", C * h, C * h + C), ou))
+        tc(A("kai", 0, 64), I(A("kr", 0, C), ou))
+        ts(A("pm", 0, 64), I(A("gg", 0, C), ou), 192.0, O.add)
+        ts(A("qn", 0, 64), I(A("gg", C, 2 * C), ou), 192.0, O.add)
         ts(A("jm", 0, 64), A("kai", 0, 64), 15, O.bitwise_and)
+        tt(A("on", 0, 64), A("sc", 64, 128), A("sc", 0, 64), O.is_gt)
+        act(A("ht", 256, 320), A("on", 0, 64), scale=-511.0)
         ts(A("ht", 0, 64), A("kai", 0, 64), kCA0, O.is_lt)
         ts(A("pab", 0, 64), A("kai", 0, 64), kCA, O.is_ge)
         ts(A("ht", 64, 128), A("jm", 0, 64), kCB0, O.is_lt)
         ts(A("pab", 64, 128), A("jm", 0, 64), kCB, O.is_ge)
-        ts(A("ht", 256, 320), A("km", 0, 64), 0.0, O.is_lt, -511.0, O.mult)
         ts(A("ht", 320, 384), A("kai", 0, 64), 0.0, O.is_equal, float(C * 513), O.mult)
         tt(A("ht", 128, 192), A("pab", 0, 64), A("pm", 0, 64), O.mult)
-        tt(A("ht", 192, 256), A("pab", 64, 128), A("qm", 0, 64), O.mult)
+        tt(A("ht", 192, 256), A("pab", 64, 128), A("qn", 0, 64), O.mult)
         turn(A("htt", 0, 384), A("ht", 0, 384))
         scan(A("ab", 0, 128), A("htt", 0, 128), A("htt", 128, 256), O.mult, O.add)
         W = lambda k: A("w", 64 * k, 64 * k + 64)
@@ -388,8 +429,8 @@ def rank_program(g, core, T, topo):
         scan(A("ps", 0, SL), r16(SL), A("pl", 0, SL), O.mult, O.add)
         tc(A("pi3", 0, 20), A("ps", 15, SL, 16))
         ts(A("pi3", 20, 40), A("pi3", 0, 20), 511, O.bitwise_and)
-        ts(A("pi3", 40, 60), A("pi3", 0, 20), 9, O.arith_shift_right)
         tc(A("xyu", 0, 20), A("pi3", 20, 40))
+        ts(A("pi3", 40, 60), A("pi3", 0, 20), 9, O.arith_shift_right)
         tc(A("xyu", 20, 40), A("pi3", 40, 60))
         for h in range(2):
             for b in range(4):
@@ -409,20 +450,18 @@ def rank_program(g, core, T, topo):
             search_constants()
         tc(A("pri", 0, SL), A("pr", 0, SL))
         ts(A("xri", 0, SL), A("pri", 0, SL), 511, O.bitwise_and)
-        ts(A("xp", 0, SL), I(A("xri", 0, SL), A("px", 0, 20)), -192.0, O.add)
+        ts(A("xp", 0, SL), I(A("xri", 0, SL), A("pz", 20, 40)), -192.0, O.add)
         for c in list(range(VROWS, 24)) + list(range(VROWS)):
             row = A("d0e", EB * c + 2, EB * c + EB)
             if c < VROWS:
                 ts(row, A("xp", 0, SL), A("nm", c, c + 1), O.not_equal, 1024.0, O.mult)
             else:
                 act(row, A("xp", 0, SL), AF.Square, bias=A("nbias", c, c + 1), scale=32.0)
-        tt(A("k1", 0, 64), A("km", 0, 64), md(64), O.mult)
+        tt(A("k1", 0, 64), A("on", 0, 64), md(64), O.mult)
         n64 = lambda k: A("n64", 64 * k, 64 * k + 64)
         ts(n64(0), A("kai", 0, 64), 0.0, O.is_gt)
         scan(A("kl", 0, 64), r16(64), A("k1", 0, 64), O.mult, O.add)
-        if not last:
-            ts(A("tv", 0, 64), A("order", 0, 64), kM0, O.mult)
-        ts(A("po", 0, 4), A("kl", 15, 64, 16), 0.0, O.is_ge, 384.0, O.mult)
+        ts(A("po", 0, 4), A("kl", 15, 64, 16), 0.5, O.is_lt, 384.0, O.mult)
         tt(A("po", 4, 8), A("po", 0, 4), A("ol", 15, 64, 16), O.add)
         pu = A("pu", 0, 4)
         tc(pu, A("po", 4, 8))
@@ -433,15 +472,6 @@ def rank_program(g, core, T, topo):
         scatter(A("lrep", 0, 768), pu, n64(4))
         if last:
             dma("s", ext(T.ol[:, :]), (T.lrep[0:128:16, :], [("lrep", 0, 768, 1)]))
-        else:
-            ts(A("tv", 64, 128), n64(4), kML, O.mult)
-            tt(A("lx", 0, 768), A("lrep", 0, 768), md(768), O.mult)
-            tt(A("tv", 128, 192), A("tv", 64, 128), A("tv", 0, 64), O.add)
-            scan(A("lsn", 0, 768), r16(768), A("lx", 0, 768), O.mult, O.add)
-            scatter(A("ltyp", 0, 768), pu, A("tv", 128, 192))
-            tc(A("ll", 0, 48), A("lsn", 15, 768, 16))
-            tc(A("lu", 0, 48), A("lsn", 15, 768, 16))
-            tt(A("dl", 0, 24), A("ll", 24, 48), A("ll", 0, 24), O.subtract)
         for k in range(4):
             a, e = 6 * EB * k, 6 * EB * k + 6 * EB
             scan(A("ste", a, e), A("d0e", a, e), A("one6", 0, 6 * EB), O.min, O.add)

@@ -2,15 +2,14 @@ from concourse.mybir import dt, AluOpType as O, ActivationFunctionType as AF
 
 N, C, L, M, R = 4, 384, 5, 64, 3
 SL = L * M
-HALF = SL // 2
 PAIRS = sorted(((i + j, i, j) for i in range(L) for j in range(L)))
 NB = len(PAIRS) + 1
 EB = SL + 2
 BIG = 1e29
 UP = 1024.0
 CUT = 224
-VROWS = 8
-AROWS = (20, 19)
+VROWS = 10
+AROWS = (20, 19, 18)
 TILES = [(rows, max(128, 16 * min(max(rows), 24))) for rows in ([24, 23, 22, 21], [20, 19, 18, 17], [16, 15, 14, 13],
                                                               [12, 11, 10, 9], [8, 7, 6, 5], [4, 3, 2, 1])]
 
@@ -33,16 +32,20 @@ def _pool(pool, dtype, spec):
     SCRATCH[pool] = ("sbuf", [128, at], dtype)
 
 
-_own(BF, "x0:1536 x1:1536 x2:1536 x3:1536 ut:512 vt:512 et:2048 ones:512 za:1280 zt0:640 zt1:640")
+_own(BF, "x0:1536 x1:1536 x2:1536 x3:1536 ut:512 vt:512 et:2048 ones:512 za:1280 zt:1280")
 _own(BF, "fb0:384 fb1:384 fb2:384 fb3:384 db0:400 db1:400 db2:400 db3:400 bd:512 bd1:512 mt:5632")
 _own(F32, "hs0:328 hs1:328 hs2:328 hs3:328 lrep:768 ys:384")
 _own(I32, "nbl:48 nbw:768")
-for _n, _k in (("w", 512), ("v", 128), ("u0", 128), ("u", 128), ("e", 512), ("x", 384), ("bd", 128), ("m", 1408)):
+for _n, _k in (("w", 512), ("v", 128), ("u0", 128), ("u", 128), ("e", 512), ("z", 320), ("bd", 128), ("m", 1408)):
     _own(COD, "q%s:%d" % (_n, _k))
     _own("uint8", "s%s:%d" % (_n, _k))
 for _t in range(R):
-    _own(COD, "zc%d:320 lc%d:320" % (_t, _t))
-    _own("uint8", "zs%d:320 ls%d:320" % (_t, _t))
+    _own(COD, "lc%d:384" % _t)
+    _own("uint8", "ls%d:384" % _t)
+    _own(U16, "own%d:40 came%d:40" % (_t, _t))
+for _t in range(R + 1):
+    _own(COD, "qx%d:384" % _t)
+    _own("uint8", "sx%d:384" % _t)
 _pool("poolf", F32, "jm16:768 jz:768 jy:768 md:384 r16:384 da:768 db:768 mk:384 d0f:384 idr:384 b0:384 col:32 nl:24 nm:24 "
       "nbias:24 cc:40 cd:40 ce:40 ll:48 l2:48 dl:24 la:768 lb:768 smd:384 sn:384 ssb:384 sp:768 fl:24 fx:24 ix:24 cm:24 "
       "cl:24 v0:384 v1:384 v2:384 v3:384 vb:384 npos:24 rk2:24 cx:384 cs:384 ms:384 mi:384 ff:384 cnt:24 rk:24 order:384 "
@@ -51,13 +54,14 @@ _pool("poolf", F32, "jm16:768 jz:768 jy:768 md:384 r16:384 da:768 db:768 mk:384 
 _pool("poolb", BF, "gg:768 gt:768 r16b:384 d1k:624 one6:1932 ne:624 st:624 ex:384 kr:384 tm:384 sg:1536 eqs:384 "
       "junk:1536 xp:320 d0e:7728")
 _pool("pooli", I32, "pi:2 li:48 li2:24 li3:20 li4:24 li5:8 ca:40 cb:40 kai:64 jm:64 pi3:60 pri:320 xri:320")
-_pool("poolu", U16, "upl:8 inl:48 exr:24 exp:20 pz:40 lu:48 ixu:24 cu:24 rku:24 ou:4 xyu:40 eu:24 pu:4")
+_pool("poolu", U16, "upl:8 inl:48 exr:24 exp:20 pz:40 lu:48 ixu:24 cu:24 rku:24 ou:4 eu:24 pu:4")
 _pool("poolh", F16, "ste:7728")
 PSUM = ("pS", "pC", "pF0", "pF1", "pF2", "pF3")
 for _n in PSUM:
     SCRATCH[_n] = ("psum", [128, 512], F32)
 NDMA = 40
-SEMAPHORES = ["qv_", "qa_", "qt_", "qp_", "lsent"] + ["ar%d" % t for t in range(R)] + ["d%d" % k for k in range(NDMA)]
+SEMAPHORES = (["qv_", "qa_", "qt_", "qp_", "lsent"] + ["arx%d" % t for t in range(R)] + ["arl%d" % t for t in range(R)]
+              + ["d%d" % k for k in range(NDMA)])
 
 
 def rank_program(g, core, T, topo):
@@ -123,6 +127,10 @@ def rank_program(g, core, T, topo):
         count[src] = 16
         clocks[(src, 16)] = {**known[q], src: 16}
         note(src, 16, in_[1], out[1])
+
+    def send(out, in_, sem):
+        order("p", in_[1], [])
+        g.remote_dma(out, in_[0], T.sem[sem], T.sem.lsent, pid, rid, mask)
 
     def A(n, a, b, s=1):
         buf, o = PLACE.get(n, (n, 0))
@@ -223,17 +231,20 @@ def rank_program(g, core, T, topo):
     iota(A("idr", 0, C), [[1, C]], 0, 0, True)
     iota(A("li3", 0, 20), [[1, 5], [16, 4]], 0, 0)
     iota(A("li4", 0, 24), [[NB, 24]], NB - 1, 0)
-    for b in range(4):
-        iota(A("db%d" % b, C, C + 16), [[0, 16]], 0, 0, True)
-    ones, half, blocks = A("ones", 0, 512), A("bd1", 0, 512), A("bd", 0, 512)
-    iota(ones, [[0, 512]], 1, 0, True)
-    for b in range(4):
-        choose(A("et", 512 * b, 512 * b + 512), ones, [[4, 128], [1, 4]], O.is_equal, -b, -4)
-    choose(half, ones, [[-16, 8], [0, 64]], O.is_ge, 0, 1)
-    choose(blocks, half, [[16, 8], [0, 64]], O.is_ge, 15, -1)
-    for b in range(4):
-        iota(A("hs%d" % b, SL, SL + 8), [[0, 8]], 0, 0, True)
-    iota(A("one6", 0, 6 * EB), [[0, 6 * EB]], 1, 0, True)
+
+    def tile_constants():
+        for b in range(4):
+            iota(A("db%d" % b, C, C + 16), [[0, 16]], 0, 0, True)
+        ones, half, blocks = A("ones", 0, 512), A("bd1", 0, 512), A("bd", 0, 512)
+        iota(ones, [[0, 512]], 1, 0, True)
+        for b in range(4):
+            choose(A("et", 512 * b, 512 * b + 512), ones, [[4, 128], [1, 4]], O.is_equal, -b, -4)
+        choose(half, ones, [[-16, 8], [0, 64]], O.is_ge, 0, 1)
+        choose(blocks, half, [[16, 8], [0, 64]], O.is_ge, 15, -1)
+        for b in range(4):
+            iota(A("hs%d" % b, SL, SL + 8), [[0, 8]], 0, 0, True)
+        iota(A("one6", 0, 6 * EB), [[0, 6 * EB]], 1, 0, True)
+
     ts(A("pi", 1, 2), A("pi", 0, 1), 15, O.bitwise_and)
     tc(A("upl", 0, 8), A("li5", 0, 8))
     tc(kI, A("pi", 1, 2))
@@ -259,11 +270,20 @@ def rank_program(g, core, T, topo):
     tc(U32("qu", 0, 128), I(U32("qu0", 0, 128), A("upl", 0, 8)))
     tc(A("su", 0, 128), I(A("su0", 0, 128), A("upl", 0, 8)))
 
-    qx, sx, S = A("qx", 0, C), A("sx", 0, C), A("pS", 0, C)
+    S = A("pS", 0, C)
 
     def scores(t):
+        qx, sx = A("qx%d" % t, 0, C), A("sx%d" % t, 0, C)
         quant(qx, sx, A("x%d" % t, 0, 4 * C))
         mm(S, A("qu", 0, 128), A("su", 0, 128), qx, sx)
+        send(T["lc%d" % t][:, 0:C].bitcast(dt.uint8), U8("qx%d" % t, 0, C), "arx%d" % t)
+        send(T["ls%d" % t][:, 0:C], sx, "arx%d" % t)
+        note("arx%d" % t, 2 * width, [], [("lc%d" % t, 0, C, 1), ("ls%d" % t, 0, C, 1)])
+        return qx, sx
+
+    def planes(codes, plane):
+        for b in range(4):
+            mm(A("pF%d" % b, 0, C), A("qe", 128 * b, 128 * b + 128), A("se", 128 * b, 128 * b + 128), codes, plane)
 
     def late_constants():
         quant(A("qe", 0, 512), A("se", 0, 512), A("et", 0, 2048))
@@ -278,7 +298,7 @@ def rank_program(g, core, T, topo):
             if steps[e] != most:
                 fill(A("d1k", e, 24 * NB, NB), float(steps[e]))
         fill(A("ne", 0, 24 * NB, NB), 0.0)
-        quant(A("qbd", 0, 128), A("sbd", 0, 128), blocks)
+        quant(A("qbd", 0, 128), A("sbd", 0, 128), A("bd", 0, 512))
         fill(A("cnt", 0, 1), 0.0)
         at = 0
         for rows, w in TILES:
@@ -313,7 +333,9 @@ def rank_program(g, core, T, topo):
 
     for t in range(R):
         last = t == R - 1
-        scores(t)
+        qx, sx = scores(t)
+        if t == 0:
+            tile_constants()
         if t == 0:
             tc(A("lrep", 0, 768), I(nbw, A("inl", 0, 48)))
             tc(A("ll", 0, 48), A("nbl", 0, 48))
@@ -344,14 +366,12 @@ def rank_program(g, core, T, topo):
         ts(A("gg", C, 2 * C), I(A("v3", 0, C), A("lu", 24, 48)), kOff, O.add)
         if t == 0:
             late_constants()
-        for b in range(4):
-            mm(A("pF%d" % b, 0, C), A("qe", 128 * b, 128 * b + 128), A("se", 128 * b, 128 * b + 128), qx, sx)
+        planes(qx, sx)
         turn(A("gt", C, 2 * C), A("gg", C, 2 * C))
         turn(A("gt", 0, C), A("gg", 0, C))
         act(A("sp", 0, 768), I(A("ssb", 0, C), A("lu", 0, 48)))
         for b in range(4):
             act(A("fb%d" % b, 0, C), A("pF%d" % b, 0, C))
-            act(A("db%d" % b, 0, C), A("pF%d" % b, 0, C), scale=0.5)
         p = lambda i: A("gt", i, C, 16)
         q = lambda j: A("gt", C + j, 2 * C, 16)
         for r in range(len(PAIRS)):
@@ -429,42 +449,44 @@ def rank_program(g, core, T, topo):
         scan(A("ps", 0, SL), r16(SL), A("pl", 0, SL), O.mult, O.add)
         tc(A("pi3", 0, 20), A("ps", 15, SL, 16))
         ts(A("pi3", 20, 40), A("pi3", 0, 20), 511, O.bitwise_and)
-        tc(A("xyu", 0, 20), A("pi3", 20, 40))
         ts(A("pi3", 40, 60), A("pi3", 0, 20), 9, O.arith_shift_right)
-        tc(A("xyu", 20, 40), A("pi3", 40, 60))
-        for h in range(2):
-            for b in range(4):
-                z = A("za", HALF * (4 * h + b), HALF * (4 * h + b + 1))
-                win = A("db%d" % b, 0, C + 16)
-                act(z, I(win, A("xyu", 10 * h, 10 * h + 10)))
-                tt(A("zt%d" % h, b, 4 * HALF, 4), I(win, A("xyu", 20 + 10 * h, 30 + 10 * h)), z, O.add)
-            a, e = HALF * h, HALF * h + HALF
-            quant(A("zc%d" % t, a, e), A("zs%d" % t, a, e), A("zt%d" % h, 0, 4 * HALF))
-            order("p", [("zc%d" % t, a, e, 1), ("zs%d" % t, a, e, 1)], [])
-            g.remote_dma(T["lc%d" % t][:, a:e].bitcast(dt.uint8), T["zc%d" % t][:, a:e].bitcast(dt.uint8),
-                         T.sem["ar%d" % t], T.sem.lsent, pid, rid, mask)
-            g.remote_dma(T["ls%d" % t][:, a:e], T["zs%d" % t][:, a:e],
-                         T.sem["ar%d" % t], T.sem.lsent, pid, rid, mask)
-        note("ar%d" % t, 4 * width, [], [("lc%d" % t, 0, SL, 1), ("ls%d" % t, 0, SL, 1)])
+        tc(A("own%d" % t, 0, 20), A("pi3", 20, 40))
+        tc(A("own%d" % t, 20, 40), A("pi3", 40, 60))
+        send(T["came%d" % t][:, 0:40], A("own%d" % t, 0, 40), "arl%d" % t)
+        note("arl%d" % t, width, [], [("came%d" % t, 0, 40, 1)])
+        planes(A("lc%d" % t, 0, C), A("ls%d" % t, 0, C))
+        for b in range(4):
+            act(A("db%d" % b, 0, C), A("pF%d" % b, 0, C), scale=0.5)
         if t == 0:
             search_constants()
         tc(A("pri", 0, SL), A("pr", 0, SL))
-        ts(A("xri", 0, SL), A("pri", 0, SL), 511, O.bitwise_and)
-        ts(A("xp", 0, SL), I(A("xri", 0, SL), A("pz", 20, 40)), -192.0, O.add)
-        for c in list(range(VROWS, 24)) + list(range(VROWS)):
-            row = A("d0e", EB * c + 2, EB * c + EB)
-            if c < VROWS:
-                ts(row, A("xp", 0, SL), A("nm", c, c + 1), O.not_equal, 1024.0, O.mult)
-            else:
-                act(row, A("xp", 0, SL), AF.Square, bias=A("nbias", c, c + 1), scale=32.0)
         tt(A("k1", 0, 64), A("on", 0, 64), md(64), O.mult)
-        n64 = lambda k: A("n64", 64 * k, 64 * k + 64)
-        ts(n64(0), A("kai", 0, 64), 0.0, O.is_gt)
+        ts(A("xri", 0, SL), A("pri", 0, SL), 511, O.bitwise_and)
         scan(A("kl", 0, 64), r16(64), A("k1", 0, 64), O.mult, O.add)
-        ts(A("po", 0, 4), A("kl", 15, 64, 16), 0.5, O.is_lt, 384.0, O.mult)
-        tt(A("po", 4, 8), A("po", 0, 4), A("ol", 15, 64, 16), O.add)
-        pu = A("pu", 0, 4)
-        tc(pu, A("po", 4, 8))
+        ts(A("xp", 0, SL), I(A("xri", 0, SL), A("pz", 20, 40)), -192.0, O.add)
+        for c in range(VROWS, 24):
+            act(A("d0e", EB * c + 2, EB * c + EB), A("xp", 0, SL), AF.Square, bias=A("nbias", c, c + 1), scale=32.0)
+        n64, pu = lambda k: A("n64", 64 * k, 64 * k + 64), A("pu", 0, 4)
+        between = [lambda: ts(A("po", 0, 4), A("kl", 15, 64, 16), 0.5, O.is_lt, 384.0, O.mult),
+                   lambda: tt(A("po", 4, 8), A("po", 0, 4), A("ol", 15, 64, 16), O.add),
+                   lambda: tc(pu, A("po", 4, 8)),
+                   lambda: ts(n64(0), A("kai", 0, 64), 0.0, O.is_gt)]
+        for c in range(VROWS):
+            ts(A("d0e", EB * c + 2, EB * c + EB), A("xp", 0, SL), A("nm", c, c + 1), O.not_equal, 1024.0, O.mult)
+            if c < len(between):
+                between[c]()
+        for k in range(4):
+            a, e = 6 * EB * k, 6 * EB * k + 6 * EB
+            scan(A("ste", a, e), A("d0e", a, e), A("one6", 0, 6 * EB), O.min, O.add)
+        ts(A("eu", 0, 24), A("ste", EB - 1, 24 * EB, EB), -1.0, O.add)
+        for b in range(4):
+            z, win = A("za", SL * b, SL * b + SL), A("db%d" % b, 0, C + 16)
+            act(z, I(win, A("came%d" % t, 0, 20)))
+            tt(A("zt", b, 4 * SL, 4), I(win, A("came%d" % t, 20, 40)), z, O.add)
+        quant(A("qz", 0, SL), A("sz", 0, SL), A("zt", 0, 4 * SL))
+        for b in range(4):
+            mm(A("pF%d" % b, 0, SL), A("qw", 128 * b, 128 * b + 128), A("sw", 128 * b, 128 * b + 128),
+               A("qz", 0, SL), A("sz", 0, SL))
         tc(n64(1), I(A("lrep", 0, 768), pu))
         tt(n64(2), A("xri", 4 * M, 5 * M), n64(1), O.subtract)
         tt(n64(3), n64(2), n64(0), O.mult)
@@ -472,26 +494,21 @@ def rank_program(g, core, T, topo):
         scatter(A("lrep", 0, 768), pu, n64(4))
         if last:
             dma("s", ext(T.ol[:, :]), (T.lrep[0:128:16, :], [("lrep", 0, 768, 1)]))
-        for k in range(4):
-            a, e = 6 * EB * k, 6 * EB * k + 6 * EB
-            scan(A("ste", a, e), A("d0e", a, e), A("one6", 0, 6 * EB), O.min, O.add)
-        ts(A("eu", 0, 24), A("ste", EB - 1, 24 * EB, EB), -1.0, O.add)
-        for b in range(4):
-            mm(A("pF%d" % b, 0, SL), A("qw", 128 * b, 128 * b + 128), A("sw", 128 * b, 128 * b + 128),
-               A("lc%d" % t, 0, SL), A("ls%d" % t, 0, SL))
         for b in range(4):
             act(A("hs%d" % b, 0, SL), A("pF%d" % b, 0, SL), scale=0.03125)
             tt(A("x%d" % (t + 1), b, 4 * C, 4), I(A("hs%d" % b, 0, SL + 8), A("eu", 0, 24)), A("fb%d" % b, 0, C), O.add)
 
+    qx, sx = A("qx%d" % R, 0, C), A("sx%d" % R, 0, C)
     quant(qx, sx, A("x%d" % R, 0, 4 * C))
     mm(S, A("qv", 0, 128), A("sv", 0, 128), qx, sx)
-    dma("s", ext(T.oc[:, :]), U8("qx", 0, C))
+    dma("s", ext(T.oc[:, :]), U8("qx%d" % R, 0, C))
     for k in range(4):
-        dma("as"[k % 2], ext(T.osc[4 * k:4 * k + 4, :]), (T.sx[32 * k:32 * k + 4, 0:C], sx[1]))
+        dma("as"[k % 2], ext(T.osc[4 * k:4 * k + 4, :]), (T["sx%d" % R][32 * k:32 * k + 4, 0:C], sx[1]))
     act(A("ys", 0, C), S)
     dma("a", ext(T.y[:, :]), A("ys", 0, C))
     for src in sorted(count):
         need("p", src, count[src])
-    g.wait_ge(T.sem.lsent, R * 4 * width)
+    g.wait_ge(T.sem.lsent, R * 3 * width)
     for t in range(R):
-        need("p", "ar%d" % t, 4 * width)
+        need("p", "arx%d" % t, 2 * width)
+        need("p", "arl%d" % t, width)

from concourse.mybir import dt, AluOpType as O, ActivationFunctionType as AF

N, C, L, M, R = 4, 384, 5, 64, 3
SL = L * M
PAIRS = sorted(((i + j, i, j) for i in range(L) for j in range(L)))
NB = len(PAIRS) + 1
EB = SL + 2
BIG = 1e29
UP = 1024.0
CUT = 224
VROWS = 10
AROWS = (20, 19, 18)
TILES = [(rows, max(128, 16 * min(max(rows), 24))) for rows in ([24, 23, 22, 21], [20, 19, 18, 17], [16, 15, 14, 13],
                                                              [12, 11, 10, 9], [8, 7, 6, 5], [4, 3, 2, 1])]

F32, BF, I32, U16, F16, COD = "float32", "bfloat16", "int32", "uint16", "float16", "float8_e4m3fn_x4"
SCRATCH, PLACE = {}, {}


def _own(dtype, spec):
    for item in spec.split():
        name, cols = item.split(":")
        SCRATCH[name] = ("sbuf", [128, int(cols)], dtype)


def _pool(pool, dtype, spec):
    at = 0
    for item in spec.split():
        name, cols = item.split(":")
        PLACE[name] = (pool, at)
        at += (int(cols) + 31) // 32 * 32
    SCRATCH[pool] = ("sbuf", [128, at], dtype)


_own(BF, "x0:1536 x1:1536 x2:1536 x3:1536 ut:512 vt:512 et:2048 ones:512 za:1280 zt:1280")
_own(BF, "fb0:384 fb1:384 fb2:384 fb3:384 db0:400 db1:400 db2:400 db3:400 bd:512 bd1:512 mt:5632")
_own(F32, "hs0:328 hs1:328 hs2:328 hs3:328 lrep:768 ys:384")
_own(I32, "nbl:48 nbw:768")
for _n, _k in (("w", 512), ("v", 128), ("u0", 128), ("u", 128), ("e", 512), ("z", 320), ("bd", 128), ("m", 1408)):
    _own(COD, "q%s:%d" % (_n, _k))
    _own("uint8", "s%s:%d" % (_n, _k))
for _t in range(R):
    _own(COD, "lc%d:384" % _t)
    _own("uint8", "ls%d:384" % _t)
    _own(U16, "own%d:40 came%d:40" % (_t, _t))
for _t in range(R + 1):
    _own(COD, "qx%d:384" % _t)
    _own("uint8", "sx%d:384" % _t)
_pool("poolf", F32, "jm16:768 jz:768 jy:768 md:384 r16:384 da:768 db:768 mk:384 d0f:384 idr:384 b0:384 col:32 nl:24 nm:24 "
      "nbias:24 cc:40 cd:40 ce:40 ll:48 l2:48 dl:24 la:768 lb:768 smd:384 sn:384 ssb:384 sp:768 fl:24 fx:24 ix:24 cm:24 "
      "cl:24 v0:384 v1:384 v2:384 v3:384 vb:384 npos:24 rk2:24 cx:384 cs:384 ms:384 mi:384 ff:384 cnt:24 rk:24 order:384 "
      "o1:64 ol:64 pm:64 qn:64 sc:128 on:64 pab:128 ht:384 htt:384 ab:128 w:320 pp:64 pe:320 pr:320 pl:320 ps:320 k1:64 "
      "kl:64 po:8 n64:320")
_pool("poolb", BF, "gg:768 gt:768 r16b:384 d1k:624 one6:1932 ne:624 st:624 ex:384 kr:384 tm:384 sg:1536 eqs:384 "
      "junk:1536 xp:320 d0e:7728")
_pool("pooli", I32, "pi:2 li:48 li2:24 li3:20 li4:24 li5:8 ca:40 cb:40 kai:64 jm:64 pi3:60 pri:320 xri:320")
_pool("poolu", U16, "upl:8 inl:48 exr:24 exp:20 pz:40 lu:48 ixu:24 cu:24 rku:24 ou:4 eu:24 pu:4")
_pool("poolh", F16, "ste:7728")
PSUM = ("pS", "pC", "pF0", "pF1", "pF2", "pF3")
for _n in PSUM:
    SCRATCH[_n] = ("psum", [128, 512], F32)
NDMA = 40
SEMAPHORES = (["qv_", "qa_", "qt_", "qp_", "lsent"] + ["arx%d" % t for t in range(R)] + ["arl%d" % t for t in range(R)]
              + ["d%d" % k for k in range(NDMA)])


def rank_program(g, core, T, topo):
    rank = T.rank_of(core)
    if rank is None:
        return
    nxt = T.cores[(rank + 1) % N]
    rid, pid = topo.addr(nxt)[:2]
    mask, width = topo.mask(core, nxt), len(topo.engines(core, nxt))

    eng = {"v": g.vector, "a": g.scalar, "t": g.tensor, "p": g, "s": g.sync}
    semof = {"v": "qv_", "a": "qa_", "t": "qt_", "p": "qp_"}
    count, known = {}, {q: {} for q in eng}
    clocks, hist = {}, {}
    ndma = [0]

    def need(q, src, val):
        if known[q].get(src, 0) >= val:
            return
        eng[q].wait_ge(T.sem[src], val)
        for s, n in clocks.get((src, val), {src: val}).items():
            if n > known[q].get(s, 0):
                known[q][s] = n

    def meet(x, y):
        return x[0] < y[1] and y[0] < x[1] and not (x[2] == y[2] and (x[0] - y[0]) % x[2])

    def covers(x, y):
        return x[0] <= y[0] and y[1] <= x[1] and (x[2] == 1 or x[2] == y[2] and (x[0] - y[0]) % x[2] == 0)

    def order(q, reads, writes):
        todo = {}
        mine = semof.get(q)
        for r, w in [(r, False) for r in reads] + [(r, True) for r in writes]:
            for piece, src, val, wrote in hist.get(r[0], ()):
                if meet(r[1:], piece) and (w or wrote or (r[0] in PSUM and src != mine)):
                    todo[src] = max(todo.get(src, 0), val)
        for src in sorted(todo, key=lambda s: s != mine):
            need(q, src, todo[src])

    def note(src, val, reads, writes):
        for r in writes:
            h = [x for x in hist.get(r[0], ()) if not covers(r[1:], x[0])]
            hist[r[0]] = h + [(r[1:], src, val, True)]
        for r in reads:
            if r not in writes:
                h = [x for x in hist.get(r[0], ()) if not (x[0] == r[1:] and x[1] == src and not x[3])]
                hist[r[0]] = h + [(r[1:], src, val, False)]

    def emit(q, fn, reads, writes):
        order(q, reads, writes)
        src = semof[q]
        count[src] = count.get(src, 0) + 1
        fn().then_inc(T.sem[src], 1)
        clocks[(src, count[src])] = {**known[q], src: count[src]}
        note(src, count[src], reads, writes)

    def dma(q, out, in_):
        order(q, in_[1], out[1])
        src = "d%d" % ndma[0]
        ndma[0] += 1
        eng[q].dma_start(out[0], in_[0]).then_inc(T.sem[src], 16)
        count[src] = 16
        clocks[(src, 16)] = {**known[q], src: 16}
        note(src, 16, in_[1], out[1])

    def send(out, in_, sem):
        order("p", in_[1], [])
        g.remote_dma(out, in_[0], T.sem[sem], T.sem.lsent, pid, rid, mask)

    def A(n, a, b, s=1):
        buf, o = PLACE.get(n, (n, 0))
        return (T[buf][:, o + a:o + b:s] if s > 1 else T[buf][:, o + a:o + b], [(n, a, b, s)])

    def U8(n, a, b):
        return (T[n][:, a:b].bitcast(dt.uint8), [(n, a, b, 1)])

    def U32(n, a, b):
        return (T[n][:, a:b].bitcast(dt.uint32), [(n, a, b, 1)])

    def I(win, off):
        return (win[0].indirect(off[0]), win[1] + off[1])

    def ext(v):
        return (v, [])

    def ap(x):
        return x[0] if isinstance(x, tuple) else x

    def rd(*xs):
        return [r for x in xs if isinstance(x, tuple) for r in x[1]]

    V = g.vector

    def tc(out, in_):
        emit("v", lambda: V.tensor_copy(out[0], in_[0]), rd(in_), out[1])

    def scatter(win, off, in_):
        emit("v", lambda: V.tensor_copy(win[0].indirect(off[0]), in_[0]), rd(off, in_), win[1])

    def tt(out, a, b, op):
        emit("v", lambda: V.tensor_tensor(out[0], a[0], b[0], op), rd(a, b), out[1])

    def ts(out, a, s1, op0, s2=None, op1=None):
        if op1 is None:
            emit("v", lambda: V.tensor_scalar(out[0], a[0], ap(s1), None, op0), rd(a, s1), out[1])
        else:
            emit("v", lambda: V.tensor_scalar(out[0], a[0], ap(s1), ap(s2), op0, op1), rd(a, s1, s2), out[1])

    def scan(out, d0, d1, op0, op1):
        emit("v", lambda: V.tensor_tensor_scan(out[0], d0[0], d1[0], 0.0, op0, op1), rd(d0, d1), out[1])

    def turn(out, in_):
        emit("v", lambda: V.transpose(out[0], in_[0]), rd(in_), out[1])

    def fill(out, k):
        emit("v", lambda: V.memset(out[0], k), [], out[1])

    def quant(q, s, x):
        emit("v", lambda: V.quantize_mx(q[0], s[0], x[0]), rd(x), q[1] + s[1])

    def act(out, in_, func=AF.Copy, bias=None, scale=None, accum=None):
        kw = {}
        if bias is not None:
            kw["bias"] = ap(bias)
        if scale is not None:
            kw["scale"] = ap(scale)
        if accum is not None:
            kw["accum_out"] = accum[0]
        emit("a", lambda: g.scalar.activation(out[0], in_[0], func, **kw), rd(in_, bias, scale),
             out[1] + (accum[1] if accum is not None else []))

    def mm(out, w, ws, x, xs, start=True, stop=True):
        emit("t", lambda: g.tensor.matmul_mx(out[0], w[0], ws[0], x[0], xs[0], start, stop), rd(w, ws, x, xs),
             out[1] if start else [])
        if not start:
            note(semof["t"], count[semof["t"]], [], [("pC", 0, C, 1)])

    def iota(out, pattern, base, cm, flag=False):
        kw = {"allow_small_or_imprecise_dtypes": True} if flag else {}
        emit("p", lambda: g.iota(out[0], pattern, base, cm, **kw), [], out[1])

    def choose(out, in_, pattern, cmp, base, cm):
        emit("p", lambda: g.affine_select(out[0], in_[0], pattern, cmp, 0.0, base, cm), in_[1], out[1])

    (kI, kM0, kMU, kL0, kL1, kL2, kU0, kU1, kU2, kOff, kCA, kCA0, kCB, kCB0, kI48, kT, knot15) = [
        A("col", k, k + 1) for k in range(17)]
    md, r16 = lambda n: A("md", 0, n), lambda n: A("r16", 0, n)

    dma("s", A("ut", 0, 512), ext(T.u[:, :]))
    dma("a", A("x0", 0, 768), ext(T.x[:, 0:768]))
    dma("s", A("x0", 768, 1536), ext(T.x[:, 768:1536]))
    dma("a", A("nbl", 0, 48), ext(T.nb[:, :]))
    rows = [("nbw%d" % i, 0, 768, 1) for i in range(16)]
    for i in range(16):
        dma("sa"[i % 2], (T.nbw[i:128:16, :], [rows[i]]), ext(T.nb[:, :]))
    nbw = (T.nbw[:, 0:768], rows)
    dma("s", U8("qw", 0, 512), ext(T.wc[:, :]))
    dma("s", A("sw", 0, 512), ext(T.ws[:, :]))
    dma("s", A("vt", 0, 512), ext(T.v[:, :]))

    iota(A("pi", 0, 1), [[1, 1]], 0, 1)
    iota(A("li5", 0, 8), [[16, 8]], 0, 0)
    iota(A("li2", 0, 24), [[16, 24]], 0, 0)
    iota(A("li", 0, 48), [[1, 48]], 0, 0)
    iota(A("jm16", 0, 768), [[0, 48], [1, 16]], 0, 0, True)
    iota(A("idr", 0, C), [[1, C]], 0, 0, True)
    iota(A("li3", 0, 20), [[1, 5], [16, 4]], 0, 0)
    iota(A("li4", 0, 24), [[NB, 24]], NB - 1, 0)

    def tile_constants():
        for b in range(4):
            iota(A("db%d" % b, C, C + 16), [[0, 16]], 0, 0, True)
        ones, half, blocks = A("ones", 0, 512), A("bd1", 0, 512), A("bd", 0, 512)
        iota(ones, [[0, 512]], 1, 0, True)
        for b in range(4):
            choose(A("et", 512 * b, 512 * b + 512), ones, [[4, 128], [1, 4]], O.is_equal, -b, -4)
        choose(half, ones, [[-16, 8], [0, 64]], O.is_ge, 0, 1)
        choose(blocks, half, [[16, 8], [0, 64]], O.is_ge, 15, -1)
        for b in range(4):
            iota(A("hs%d" % b, SL, SL + 8), [[0, 8]], 0, 0, True)
        iota(A("one6", 0, 6 * EB), [[0, 6 * EB]], 1, 0, True)

    ts(A("pi", 1, 2), A("pi", 0, 1), 15, O.bitwise_and)
    tc(A("upl", 0, 8), A("li5", 0, 8))
    tc(kI, A("pi", 1, 2))
    ts(kM0, kI, 0.0, O.is_equal)
    ts(kCB, kI, 1.0, O.add)
    ts(kI48, kI, 48.0, O.mult)
    ts(kMU, kI, 0.0, O.is_equal, UP, O.mult)
    act(A("jz", 0, C), A("jm16", 0, C), AF.Square, bias=kI, scale=-1.0)
    act(md(C), A("jz", 0, C), AF.Relu, bias=1.0, scale=-1.0)
    act(r16(C), A("jm16", 0, C), AF.Sign)
    act(A("b0", 0, C), A("idr", 0, C), AF.Identity, bias=kMU, scale=kM0)
    ts(A("inl", 0, 48), A("li", 0, 48), kI48, O.add)
    ts(A("nl", 0, 24), A("li2", 0, 24), kI, O.add)
    for k, (stay, up) in enumerate(((kL0, kU0), (kL1, kU1), (kL2, kU2))):
        ts(stay, kI, k + 1.5, O.is_lt)
        ts(up, kI, k + 1.5, O.is_lt, UP, O.mult)
    ts(kT, kI, UP, O.mult, -4 * UP, O.add)
    ts(kCA, kI, 16.0, O.mult, 1.0, O.add)
    ts(kCB0, kM0, -2.0, O.mult, kCB, O.add)
    ts(kOff, kT, 0.0, O.min, -192.0, O.add)
    ts(kCA0, kM0, -2.0, O.mult, kCA, O.add)
    quant(A("qu0", 0, 128), A("su0", 0, 128), A("ut", 0, 512))
    tc(U32("qu", 0, 128), I(U32("qu0", 0, 128), A("upl", 0, 8)))
    tc(A("su", 0, 128), I(A("su0", 0, 128), A("upl", 0, 8)))

    S = A("pS", 0, C)

    def scores(t):
        qx, sx = A("qx%d" % t, 0, C), A("sx%d" % t, 0, C)
        quant(qx, sx, A("x%d" % t, 0, 4 * C))
        mm(S, A("qu", 0, 128), A("su", 0, 128), qx, sx)
        send(T["lc%d" % t][:, 0:C].bitcast(dt.uint8), U8("qx%d" % t, 0, C), "arx%d" % t)
        send(T["ls%d" % t][:, 0:C], sx, "arx%d" % t)
        note("arx%d" % t, 2 * width, [], [("lc%d" % t, 0, C, 1), ("ls%d" % t, 0, C, 1)])
        return qx, sx

    def planes(codes, plane):
        for b in range(4):
            mm(A("pF%d" % b, 0, C), A("qe", 128 * b, 128 * b + 128), A("se", 128 * b, 128 * b + 128), codes, plane)

    def late_constants():
        quant(A("qe", 0, 512), A("se", 0, 512), A("et", 0, 2048))
        tc(A("exr", 0, 24), A("li4", 0, 24))
        tc(A("exp", 0, 20), A("li3", 0, 20))
        f = [16 * i + j + 1 for _, i, j in PAIRS]
        f[0] = 0
        steps = [-f[-1]] + [f[r] - f[r - 1] for r in range(len(PAIRS) - 1, 0, -1)] + [0]
        most = max(steps, key=steps.count)
        fill(A("d1k", 0, 24 * NB), float(most))
        for e in range(NB):
            if steps[e] != most:
                fill(A("d1k", e, 24 * NB, NB), float(steps[e]))
        fill(A("ne", 0, 24 * NB, NB), 0.0)
        quant(A("qbd", 0, 128), A("sbd", 0, 128), A("bd", 0, 512))
        fill(A("cnt", 0, 1), 0.0)
        at = 0
        for rows, w in TILES:
            fill(A("mt", at + 64 * min(rows), at + 4 * w), 0.0)
            at += 4 * w
        ts(A("npos", 0, 24), A("li2", 0, 24), kI, O.subtract, 15.0, O.add)
        ts(knot15, kI, 15.0, O.is_lt)
        act(A("mk", 0, C), md(C), AF.Identity, bias=-2e29, scale=5e29)
        act(A("d0f", 0, C), r16(C), AF.Identity, bias=-2e29, scale=5e29)
        act(A("r16b", 0, C), r16(C))

    def last_constants():
        act(A("ce", 0, 20), A("nl", 0, 20))
        act(A("ce", 20, 40), A("nl", 0, 20), AF.Identity, bias=float(SL - 1), scale=-1.0)
        act(A("cd", 0, 40), A("ce", 0, 40), scale=64.0)
        ts(A("ca", 0, 40), A("ce", 0, 40), 205.0, O.mult)
        ts(A("cb", 0, 40), A("ca", 0, 40), 10, O.arith_shift_right)
        ts(A("cc", 0, 40), A("cb", 0, 40), -319.0, O.mult)
        tt(A("ce", 0, 40), A("cc", 0, 40), A("cd", 0, 40), O.add)
        tc(A("pz", 0, 40), A("ce", 0, 40))
        act(A("jz", 0, 768), A("jm16", 0, 768), AF.Square, bias=kI, scale=-1.0)
        act(A("da", 0, 768), A("jz", 0, 768), AF.Sign)
        act(A("jy", 0, 768), A("jm16", 0, 768), AF.Square, bias=kCB, scale=-1.0)
        act(A("db", 0, 768), A("jy", 0, 768), AF.Sign)

    def search_constants():
        act(A("nm", 0, 24), A("nl", 0, 24), AF.Identity, bias=-192.0)
        act(A("nbias", 0, 24), A("nl", 0, 24), AF.Identity, bias=32.0 * 192, scale=-32.0)
        fill(A("d0e", 0, 24 * EB, EB), 0.0)
        fill(A("d0e", 1, 24 * EB, EB), 0.0)
        quant(A("qv", 0, 128), A("sv", 0, 128), A("vt", 0, 512))

    for t in range(R):
        last = t == R - 1
        qx, sx = scores(t)
        if t == 0:
            tile_constants()
        if t == 0:
            tc(A("lrep", 0, 768), I(nbw, A("inl", 0, 48)))
            tc(A("ll", 0, 48), A("nbl", 0, 48))
        else:
            scan(A("la", 0, 768), A("da", 0, 768), A("lrep", 0, 768), O.mult, O.add)
            scan(A("lb", 0, 768), A("db", 0, 768), A("lrep", 0, 768), O.mult, O.add)
            ts(A("l2", 0, 48), A("lb", 15, 768, 16), knot15, O.mult)
            tt(A("ll", 0, 48), A("la", 15, 768, 16), A("l2", 0, 48), O.subtract)
        tt(A("smd", 0, C), S, md(C), O.mult)
        act(A("ssb", 0, C), S)
        tt(A("dl", 0, 24), A("ll", 24, 48), A("ll", 0, 24), O.subtract)
        scan(A("sn", 0, C), r16(C), A("smd", 0, C), O.mult, O.add)
        sl = A("sn", 15, C, 16)
        ts(A("fx", 0, 24), sl, 0.0, O.is_gt, 384.0, O.mult)
        ts(A("fl", 0, 24), sl, 0.0, O.is_gt)
        tt(A("ix", 0, 24), A("fx", 0, 24), A("nl", 0, 24), O.add)
        tt(A("cm", 0, 24), A("fl", 0, 24), A("dl", 0, 24), O.mult)
        tc(A("ixu", 0, 24), A("ix", 0, 24))
        tt(A("cl", 0, 24), A("cm", 0, 24), A("ll", 0, 24), O.add)
        tt(A("v0", 0, C), I(A("lrep", 0, 768), A("ixu", 0, 24)), A("b0", 0, C), O.max)
        tc(A("cu", 0, 24), A("cl", 0, 24))
        tc(A("lu", 0, 48), A("ll", 0, 48))
        for k, (stay, up) in enumerate(((kL0, kU0), (kL1, kU1), (kL2, kU2))):
            act(A("vb", 0, CUT), A("v%d" % k, 0, CUT), AF.Identity, bias=up, scale=stay)
            ts(A("vb", CUT, C), A("v%d" % k, CUT, C), stay, O.mult, up, O.add)
            tt(A("v%d" % (k + 1), 0, C), I(A("v%d" % k, 0, C), A("cu", 0, 24)), A("vb", 0, C), O.max)
        act(A("gg", 0, C), I(A("v3", 0, C), A("lu", 0, 24)), AF.Identity, bias=kOff)
        ts(A("gg", C, 2 * C), I(A("v3", 0, C), A("lu", 24, 48)), kOff, O.add)
        if t == 0:
            late_constants()
        planes(qx, sx)
        turn(A("gt", C, 2 * C), A("gg", C, 2 * C))
        turn(A("gt", 0, C), A("gg", 0, C))
        act(A("sp", 0, 768), I(A("ssb", 0, C), A("lu", 0, 48)))
        for b in range(4):
            act(A("fb%d" % b, 0, C), A("pF%d" % b, 0, C))
        p = lambda i: A("gt", i, C, 16)
        q = lambda j: A("gt", C + j, 2 * C, 16)
        for r in range(len(PAIRS)):
            tt(A("ne", 25 - r, 24 * NB, NB), p(PAIRS[r][1]), q(PAIRS[r][2]), O.not_equal)
        scan(A("st", 0, 24 * NB), A("ne", 0, 24 * NB), A("d1k", 0, 24 * NB), O.mult, O.add)
        tc(A("ex", 0, C), I(A("st", 0, 24 * NB), A("exr", 0, 24)))
        turn(A("kr", 0, C), A("ex", 0, C))
        ts(A("tm", 0, C), A("kr", 0, C), 0.0, O.is_equal, -BIG, O.mult)
        tt(A("ms", 0, C), S, A("tm", 0, C), O.add)
        tt(A("mi", 0, C), A("ms", 0, C), A("mk", 0, C), O.min)
        scan(A("ff", 0, C), A("d0f", 0, C), A("mi", 0, C), O.min, O.max)
        spot, at = {}, 0
        for rows, w in TILES:
            for i, c in enumerate(rows):
                spot[c] = A("mt", at + i, at + 64 * min(c, 24), 4)
            at += 4 * w
        score = lambda c: A("ff", 16 * c + 15, 16 * c + 16)
        for c in AROWS:
            sg = A("sg", C * (c % 4), C * (c % 4) + 16 * c)
            act(sg, A("ms", 0, 16 * c), AF.Sign, bias=score(c), scale=-1.0)
            act(spot[c], sg, AF.Relu, accum=A("cnt", c, c + 1))
        at = 0
        for k, (rows, w) in enumerate(TILES):
            for c in rows:
                if c == 24:
                    tt(spot[c], A("ms", 0, C), A("ff", 0, C), O.is_le)
                    scan(A("eqs", 0, C), A("r16b", 0, C), spot[c], O.mult, O.add)
                elif c not in AROWS:
                    ts(spot[c], A("ms", 0, 16 * c), score(c), O.is_lt)
                    act(A("junk", C * (c % 4), C * (c % 4) + 16 * c), spot[c], accum=A("cnt", c, c + 1))
            a = at // 4
            quant(A("qm", a, a + w), A("sm", a, a + w), A("mt", at, at + 4 * w))
            mm(A("pC", 0, w), A("qbd", 0, 128), A("sbd", 0, 128), A("qm", a, a + w), A("sm", a, a + w), k == 0, k == 5)
            at += 4 * w
        if t == 0:
            last_constants()
        tt(A("rk", 0, 24), A("npos", 0, 24), A("eqs", 15, C, 16), O.subtract)
        tt(A("cx", 0, C), A("pC", 0, C), md(C), O.mult)
        tt(A("rk2", 0, 24), A("rk", 0, 24), A("cnt", 0, 24), O.subtract)
        scan(A("cs", 0, C), r16(C), A("cx", 0, C), O.mult, O.add)
        tt(A("rk", 0, 24), A("rk2", 0, 24), A("cs", 15, C, 16), O.add)
        tc(A("rku", 0, 24), A("rk", 0, 24))
        scatter(A("order", 0, C), A("rku", 0, 24), A("idr", 0, C))
        tt(A("o1", 0, 64), A("order", 0, 64), md(64), O.mult)
        scan(A("ol", 0, 64), r16(64), A("o1", 0, 64), O.mult, O.add)
        tc(A("ou", 0, 4), A("ol", 15, 64, 16))
        ou = A("ou", 0, 4)
        for h in range(2):
            act(A("sc", 64 * h, 64 * h + 64), I(A("sp", C * h, C * h + C), ou))
        tc(A("kai", 0, 64), I(A("kr", 0, C), ou))
        ts(A("pm", 0, 64), I(A("gg", 0, C), ou), 192.0, O.add)
        ts(A("qn", 0, 64), I(A("gg", C, 2 * C), ou), 192.0, O.add)
        ts(A("jm", 0, 64), A("kai", 0, 64), 15, O.bitwise_and)
        tt(A("on", 0, 64), A("sc", 64, 128), A("sc", 0, 64), O.is_gt)
        act(A("ht", 256, 320), A("on", 0, 64), scale=-511.0)
        ts(A("ht", 0, 64), A("kai", 0, 64), kCA0, O.is_lt)
        ts(A("pab", 0, 64), A("kai", 0, 64), kCA, O.is_ge)
        ts(A("ht", 64, 128), A("jm", 0, 64), kCB0, O.is_lt)
        ts(A("pab", 64, 128), A("jm", 0, 64), kCB, O.is_ge)
        ts(A("ht", 320, 384), A("kai", 0, 64), 0.0, O.is_equal, float(C * 513), O.mult)
        tt(A("ht", 128, 192), A("pab", 0, 64), A("pm", 0, 64), O.mult)
        tt(A("ht", 192, 256), A("pab", 64, 128), A("qn", 0, 64), O.mult)
        turn(A("htt", 0, 384), A("ht", 0, 384))
        scan(A("ab", 0, 128), A("htt", 0, 128), A("htt", 128, 256), O.mult, O.add)
        W = lambda k: A("w", 64 * k, 64 * k + 64)
        tt(W(0), A("ab", 64, 128), A("ab", 0, 64), O.subtract)
        ts(W(1), A("ab", 64, 128), 512.0, O.mult)
        tt(W(2), A("ab", 0, 64), A("htt", 320, 384), O.add)
        tt(W(3), W(0), A("htt", 256, 320), O.mult)
        tt(W(4), W(1), W(2), O.add)
        tt(A("pp", 0, 64), W(4), W(3), O.add)
        tc(A("pe", 0, SL), I(A("pp", 0, 64), A("exp", 0, 20)))
        turn(A("pr", 0, SL), A("pe", 0, SL))
        tt(A("pl", 0, SL), I(A("pr", 0, SL), A("pz", 0, 20)), md(SL), O.mult)
        scan(A("ps", 0, SL), r16(SL), A("pl", 0, SL), O.mult, O.add)
        tc(A("pi3", 0, 20), A("ps", 15, SL, 16))
        ts(A("pi3", 20, 40), A("pi3", 0, 20), 511, O.bitwise_and)
        ts(A("pi3", 40, 60), A("pi3", 0, 20), 9, O.arith_shift_right)
        tc(A("own%d" % t, 0, 20), A("pi3", 20, 40))
        tc(A("own%d" % t, 20, 40), A("pi3", 40, 60))
        send(T["came%d" % t][:, 0:40], A("own%d" % t, 0, 40), "arl%d" % t)
        note("arl%d" % t, width, [], [("came%d" % t, 0, 40, 1)])
        planes(A("lc%d" % t, 0, C), A("ls%d" % t, 0, C))
        for b in range(4):
            act(A("db%d" % b, 0, C), A("pF%d" % b, 0, C), scale=0.5)
        if t == 0:
            search_constants()
        tc(A("pri", 0, SL), A("pr", 0, SL))
        tt(A("k1", 0, 64), A("on", 0, 64), md(64), O.mult)
        ts(A("xri", 0, SL), A("pri", 0, SL), 511, O.bitwise_and)
        scan(A("kl", 0, 64), r16(64), A("k1", 0, 64), O.mult, O.add)
        ts(A("xp", 0, SL), I(A("xri", 0, SL), A("pz", 20, 40)), -192.0, O.add)
        for c in range(VROWS, 24):
            act(A("d0e", EB * c + 2, EB * c + EB), A("xp", 0, SL), AF.Square, bias=A("nbias", c, c + 1), scale=32.0)
        n64, pu = lambda k: A("n64", 64 * k, 64 * k + 64), A("pu", 0, 4)
        between = [lambda: ts(A("po", 0, 4), A("kl", 15, 64, 16), 0.5, O.is_lt, 384.0, O.mult),
                   lambda: tt(A("po", 4, 8), A("po", 0, 4), A("ol", 15, 64, 16), O.add),
                   lambda: tc(pu, A("po", 4, 8)),
                   lambda: ts(n64(0), A("kai", 0, 64), 0.0, O.is_gt)]
        for c in range(VROWS):
            ts(A("d0e", EB * c + 2, EB * c + EB), A("xp", 0, SL), A("nm", c, c + 1), O.not_equal, 1024.0, O.mult)
            if c < len(between):
                between[c]()
        for k in range(4):
            a, e = 6 * EB * k, 6 * EB * k + 6 * EB
            scan(A("ste", a, e), A("d0e", a, e), A("one6", 0, 6 * EB), O.min, O.add)
        ts(A("eu", 0, 24), A("ste", EB - 1, 24 * EB, EB), -1.0, O.add)
        for b in range(4):
            z, win = A("za", SL * b, SL * b + SL), A("db%d" % b, 0, C + 16)
            act(z, I(win, A("came%d" % t, 0, 20)))
            tt(A("zt", b, 4 * SL, 4), I(win, A("came%d" % t, 20, 40)), z, O.add)
        quant(A("qz", 0, SL), A("sz", 0, SL), A("zt", 0, 4 * SL))
        for b in range(4):
            mm(A("pF%d" % b, 0, SL), A("qw", 128 * b, 128 * b + 128), A("sw", 128 * b, 128 * b + 128),
               A("qz", 0, SL), A("sz", 0, SL))
        tc(n64(1), I(A("lrep", 0, 768), pu))
        tt(n64(2), A("xri", 4 * M, 5 * M), n64(1), O.subtract)
        tt(n64(3), n64(2), n64(0), O.mult)
        tt(n64(4), n64(3), n64(1), O.add)
        scatter(A("lrep", 0, 768), pu, n64(4))
        if last:
            dma("s", ext(T.ol[:, :]), (T.lrep[0:128:16, :], [("lrep", 0, 768, 1)]))
        for b in range(4):
            act(A("hs%d" % b, 0, SL), A("pF%d" % b, 0, SL), scale=0.03125)
            tt(A("x%d" % (t + 1), b, 4 * C, 4), I(A("hs%d" % b, 0, SL + 8), A("eu", 0, 24)), A("fb%d" % b, 0, C), O.add)

    qx, sx = A("qx%d" % R, 0, C), A("sx%d" % R, 0, C)
    quant(qx, sx, A("x%d" % R, 0, 4 * C))
    mm(S, A("qv", 0, 128), A("sv", 0, 128), qx, sx)
    dma("s", ext(T.oc[:, :]), U8("qx%d" % R, 0, C))
    for k in range(4):
        dma("as"[k % 2], ext(T.osc[4 * k:4 * k + 4, :]), (T["sx%d" % R][32 * k:32 * k + 4, 0:C], sx[1]))
    act(A("ys", 0, C), S)
    dma("a", ext(T.y[:, :]), A("ys", 0, C))
    for src in sorted(count):
        need("p", src, count[src])
    g.wait_ge(T.sem.lsent, R * 3 * width)
    for t in range(R):
        need("p", "arx%d" % t, 2 * width)
        need("p", "arl%d" % t, width)
